import numpy as np
import ml_dtypes


def mxq(x, axis, fmt="e4m3"):
    dtype, down = {"e4m3": (ml_dtypes.float8_e4m3fn, 7), "e5m2": (ml_dtypes.float8_e5m2, 14)}[fmt]
    v = np.moveaxis(np.asarray(x, np.float32).astype(ml_dtypes.bfloat16).astype(np.float64), axis, -1)
    blocks = v.reshape(v.shape[:-1] + (-1, 32))
    amax = np.abs(blocks).max(-1, keepdims=True)
    byte = np.maximum(np.where(amax > 0, np.frexp(amax)[1] - 1 + 127, 0) - down, 1)
    scale = np.exp2(byte - 127.0)
    codes = (blocks / scale).astype(np.float32).astype(dtype).astype(np.float64)
    return np.moveaxis((codes * scale).reshape(v.shape), -1, axis)


WIDE = False


def mx_kscale(k):
    if not WIDE:
        return np.ones(k)
    levels = np.array([24, -24, 12, -12, 0])
    if k % 512:
        return np.exp2(np.random.permutation(np.resize(levels, k // 32))).repeat(32)
    a = np.empty((k // 512, 16))
    for p in range(k // 512):
        a[p, :8] = np.random.permutation(np.resize(levels, 8))
        for g in range(8):
            far = levels[np.abs(levels - a[p, g]) >= 10]
            a[p, g + 8] = far[np.random.randint(len(far))]
    return np.exp2(a.ravel()).repeat(32)


def f64(x):
    return np.asarray(x).astype(np.float64)


def striped(idx):
    return np.tile(idx.reshape(-1, 16).T, (8, 1)).astype(np.uint16)


def unstriped(offs):
    return offs[:16].T.reshape(-1).astype(np.int64)


E2M1 = np.array([0.0, 0.5, 1.0, 1.5, 2.0, 3.0, 4.0, 6.0, -0.0, -0.5, -1.0, -1.5, -2.0, -3.0, -4.0, -6.0])


def pack_weight(w, fmt):
    k, n = w.shape
    w = f64(np.asarray(w, np.float32).astype(ml_dtypes.bfloat16)).reshape(k // 32, 32, n)
    amax = np.abs(w).max(1)
    if fmt == "e4m3":
        byte = np.frexp(amax)[1] - 1 + 127 - 7
    else:
        mant, ex = np.frexp(amax / 6.0)
        byte = np.where(mant > 0.5, ex, ex - 1) + 127
    byte = np.clip(np.where(amax > 0, byte, 1), 1, 254)
    scaled = (w * np.exp2(127.0 - byte)[:, None, :]).reshape(k, n).astype(np.float32)
    by_word = np.ascontiguousarray(scaled.reshape(k // 512, 128, 4, n).transpose(0, 1, 3, 2))
    if fmt == "e4m3":
        words = by_word.astype(ml_dtypes.float8_e4m3fn).view(np.uint8)
    else:
        c = by_word.astype(ml_dtypes.float4_e2m1fn).view(np.uint8) & 0xF
        words = (c[..., 0::2] | (c[..., 1::2] << 4)).reshape(k // 512, 128, 2 * n)
    return np.ascontiguousarray(words), np.ascontiguousarray(byte.astype(np.uint8).reshape(k // 512, 16, n))


def unpack_weight(words, scales, fmt):
    g, _, n = scales.shape
    words = np.ascontiguousarray(words).reshape(g, 128, n, -1)
    if fmt == "e4m3":
        vals = words.view(ml_dtypes.float8_e4m3fn).astype(np.float64)
    else:
        nib = np.empty((g, 128, n, 4), np.uint8)
        nib[..., 0::2] = words & 0xF
        nib[..., 1::2] = words >> 4
        vals = E2M1[nib]
    vals = vals * np.repeat(np.exp2(scales.astype(np.float64) - 127.0), 8, axis=1)[..., None]
    return vals.transpose(0, 1, 3, 2).reshape(g * 512, n)


def pack_table4(v):
    words, scales = pack_weight(v, "e2m1")
    g, t = words.shape[0] // 2, v.shape[1]
    return np.ascontiguousarray(words.reshape(g, 2, 128, t, 2).transpose(0, 2, 3, 1, 4).reshape(g, 128, t, 4)), scales


def unpack_table4(words, scales):
    g, _, t, _ = words.shape
    return unpack_weight(words.reshape(g, 128, t, 2, 2).transpose(0, 3, 1, 2, 4).reshape(2 * g, 128, 2 * t), scales, "e2m1")


K, L, R, N, T, J = 1024, 512, 1024, 512, 2048, 1024


def setup_inputs():
    n = np.random.standard_normal
    s = mx_kscale(K)[:, None]
    s2 = mx_kscale(L)[:, None]
    u = mx_kscale(R)[:, None]
    p_tab = pack_table4(n((K, T)) * s)
    p_tab2 = pack_weight(n((L, T)) * s2, "e4m3")
    p_wa = pack_weight(n((K, R)) / np.sqrt(K) / s, "e4m3")
    p_wb = pack_weight(n((L, R)) / np.sqrt(L) / s2, "e2m1")
    p_en = pack_weight(n((R, N)) / np.sqrt(R) / u, "e2m1")
    return {
        "tab_words": p_tab[0],
        "tab_scales": p_tab[1],
        "tab2_words": p_tab2[0],
        "tab2_scales": p_tab2[1],
        "wa_words": p_wa[0],
        "wa_scales": p_wa[1],
        "wb_words": p_wb[0],
        "wb_scales": p_wb[1],
        "sm": (np.random.uniform(0.5, 2.0, R) * u[:, 0]).astype(np.float32),
        "en_words": p_en[0],
        "en_scales": p_en[1],
        "b": (0.3 * n(N)).astype(np.float32),
        "offs": striped(np.random.permutation(T)[:J]),
        "offs2": striped(np.random.permutation(T)[:J]),
    }


def reference(tab_words, tab_scales, tab2_words, tab2_scales, wa_words, wa_scales, wb_words, wb_scales, sm, en_words, en_scales, b, offs, offs2):
    idx = unstriped(offs)
    idx2 = unstriped(offs2)
    tab_ = unpack_table4(tab_words, tab_scales)[:, idx]
    tab2_ = unpack_weight(tab2_words, tab2_scales, "e4m3")[:, idx2]
    wa_ = unpack_weight(wa_words, wa_scales, "e4m3")
    wb_ = unpack_weight(wb_words, wb_scales, "e2m1")
    z = wa_.T @ tab_ + wb_.T @ tab2_
    h = f64(sm)[:, None] * np.tanh(z)
    h_ = mxq(h, 0, "e4m3")
    en_ = unpack_weight(en_words, en_scales, "e2m1")
    y = en_.T @ h_
    return y + f64(b)[:, None]

@@ -1,0 +1,226 @@
+from contextlib import ExitStack
+
+import concourse.mybir as mybir
+
+K, L, R, N, T, J = 1024, 512, 1024, 512, 2048, 1024
+FLOPS = 2 * J * R * (K + L + N)
+
+F32 = mybir.dt.float32
+BF16 = mybir.dt.bfloat16
+I32 = mybir.dt.int32
+U32 = mybir.dt.uint32
+U16 = mybir.dt.uint16
+U8 = mybir.dt.uint8
+FP8X4 = mybir.dt.float8_e4m3fn_x4
+FP4X4 = mybir.dt.float4_e2m1fn_x4
+ACT = mybir.ActivationFunctionType
+ALU = mybir.AluOpType
+
+P = 128
+W = 512
+
+
+def tile_list_kg_tanh_bias_kernel(
+    tc, tab_words, tab_scales, tab2_words, tab2_scales, wa_words, wa_scales, wb_words, wb_scales,
+    sm, en_words, en_scales, b, offs, offs2, out,
+):
+    nc = tc.nc
+    with ExitStack() as ctx:
+        keep = ctx.enter_context(tc.tile_pool(name="keep", bufs=1))
+        psum = ctx.enter_context(tc.psum_pool(name="psum", bufs=8))
+
+        def new(shape, dtype, name):
+            return keep.tile(shape, dtype, name=name, align_bytes=64)
+
+        list1 = keep.tile([P, J // 16], U16, name="list1")
+        list2 = keep.tile([P, J // 16], U16, name="list2")
+        tab_s = new([P, T // 4], I32, "tab_s")
+        tab2_s = new([P, T // 4], I32, "tab2_s")
+        w_s = new([P, R // 4], I32, "w_s")
+        en_s = new([P, 2, N // 4], I32, "en_s")
+        tab_w = new([P, T], I32, "tab_w")
+        tab2_w = new([P, T], I32, "tab2_w")
+        wa_w = [new([P, 2, W], I32, f"wa_w{a}") for a in range(2)]
+        wb_w = new([P, R // 2], I32, "wb_w")
+        en_w = new([P, 2, N // 2], I32, "en_w")
+        sm_sb = new([P, 2, 4], F32, "sm_sb")
+        b_sb = new([P, 4], F32, "b_sb")
+        warm = new([P, 1], F32, "warm")
+        g_s1 = [new([P, W // 4], I32, f"g_s1{h}") for h in range(2)]
+
+        nc.vector.memset(tab2_s[:], 0)
+        nc.vector.memset(w_s[:], 0)
+        nc.vector.memset(tab_s[:], 0)
+        nc.vector.memset(warm[:], 0.0)
+        nc.scalar.activation(out=warm[:], in_=warm[:], func=ACT.Tanh)
+
+        wa_i = wa_words.rearrange("a p r i -> p a (r i)").bitcast(I32)
+        nc.sync.dma_start(list2[:], offs2)
+        nc.sync.dma_start(list1[:], offs)
+        for q in range(4):
+            nc.sync.dma_start(tab2_s[32 * q : 32 * q + 4, :], tab2_scales[0, 4 * q : 4 * q + 4, :].bitcast(I32))
+        for q in range(4):
+            nc.sync.dma_start(w_s[32 * q : 32 * q + 4, :], wb_scales[0, 4 * q : 4 * q + 4, :].bitcast(I32))
+        for q in range(4):
+            nc.sync.dma_start(w_s[32 * q + 4 : 32 * q + 12, :], wa_scales[:, 4 * q : 4 * q + 4, :].bitcast(I32))
+        for q in range(4):
+            nc.sync.dma_start(tab_s[32 * q : 32 * q + 8, :], tab_scales[:, 4 * q : 4 * q + 4, :].bitcast(I32))
+        nc.gpsimd.dma_start(tab2_w[:], tab2_words[0].rearrange("p t i -> p (t i)").bitcast(I32))
+        nc.gpsimd.dma_start(wb_w[:], wb_words[0].bitcast(I32))
+        nc.gpsimd.dma_start(tab_w[:], tab_words[0].rearrange("p t i -> p (t i)").bitcast(I32))
+        nc.gpsimd.dma_start(wa_w[0][:], wa_i[:, :, 0:W])
+        nc.gpsimd.dma_start(wa_w[1][:], wa_i[:, :, W : 2 * W])
+        nc.gpsimd.dma_start(sm_sb[:], sm.rearrange("(a p t) -> p a t", a=2, t=4))
+        nc.gpsimd.dma_start(en_w[:], en_words.rearrange("a p n -> p a n").bitcast(I32))
+        for q in range(4):
+            nc.gpsimd.dma_start(
+                en_s[32 * q : 32 * q + 4, :, :],
+                en_scales[:, 4 * q : 4 * q + 4, :].rearrange("a r n -> r a n").bitcast(I32),
+            )
+        with nc.allow_non_contiguous_dma(reason="one bias value to a partition"):
+            nc.gpsimd.dma_start(b_sb[:], b.rearrange("(c p) -> p c", p=P))
+
+        g_s0 = [new([P, W], U8, f"g_s0{h}") for h in range(2)]
+        g_s2 = [new([P, W], U8, f"g_s2{h}") for h in range(2)]
+        g_w = [new([P, W], U32, f"g_w{h}") for h in range(2)]
+        g_w2 = [new([P, W], U32, f"g_w2{h}") for h in range(2)]
+        v_w = [new([P, 2, 2 * W], U8, f"v_w{h}") for h in range(2)]
+
+        def gather2(h):
+            cols = slice(h * W // 16, (h + 1) * W // 16)
+            nc.vector.tensor_copy(g_s2[h][:], tab2_s[:].bitcast(U8).indirect(list2[:, cols]))
+            nc.vector.tensor_copy(g_w2[h][:], tab2_w[:].bitcast(U32).indirect(list2[:, cols]))
+
+        def gather1(h):
+            cols = slice(h * W // 16, (h + 1) * W // 16)
+            nc.vector.tensor_copy(g_s0[h][:], tab_s[:].bitcast(U8).indirect(list1[:, cols]))
+            nc.sync.dma_start(g_s1[h][0:112, :], g_s0[h][4:116, :].bitcast(I32))
+            nc.vector.tensor_copy(g_w[h][:], tab_w[:].bitcast(U32).indirect(list1[:, cols]))
+
+        def part(h):
+            nc.vector.tensor_copy(
+                v_w[h][:].bitcast(U16), g_w[h][:].bitcast(U16).rearrange("p (j d) -> p d j", d=2)
+            )
+
+        wa_p = [new([P, 2, W], I32, f"wa_p{a}") for a in range(2)]
+        wb_p = new([P, 2, 2 * W], U8, "wb_p")
+        ws_p = [new([P, 2, W], U8, f"ws_p{g}") for g in range(3)]
+
+        def permute_scales():
+            nc.vector.tensor_copy(
+                ws_p[2][:].rearrange("p a (t c i) -> p a c t i", t=4, i=16),
+                w_s[:].bitcast(U8).rearrange("p (a c i t) -> p a c t i", a=2, t=4, i=16),
+            )
+            for g in range(2):
+                nc.sync.dma_start(ws_p[g][0:112].bitcast(I32), ws_p[2][4 + 4 * g : 116 + 4 * g].bitcast(I32))
+
+        def permute_wb():
+            nc.vector.tensor_copy(
+                wb_p[:].bitcast(U16).rearrange("p a (t c i) -> p a c t i", t=4, i=8),
+                wb_w[:].bitcast(U16).rearrange("p (a c i t) -> p a c t i", a=2, t=4, i=8),
+            )
+
+        def permute_wa(a):
+            nc.vector.tensor_copy(
+                wa_p[a][:].rearrange("p g (t c i) -> p g c t i", t=4, i=4),
+                wa_w[a][:].rearrange("p g (c i t) -> p g c t i", t=4, i=4),
+            )
+
+        th = {}
+        hb = {}
+        hq = {}
+        hs = {}
+        z = {}
+
+        def project2(h, a):
+            for t in range(4):
+                z[h, a, t] = psum.tile([P, W], F32, name="acc")
+                nc.tensor.matmul_mx(
+                    out=z[h, a, t][:],
+                    lhsT=wb_p[:, a, 2 * t * P : 2 * (t + 1) * P].bitcast(FP4X4),
+                    lhsT_scale=ws_p[2][:, a, t * P : (t + 1) * P],
+                    rhs=g_w2[h][:].bitcast(FP8X4),
+                    rhs_scale=g_s2[h][:],
+                    start=True,
+                    stop=False,
+                )
+
+        def project1(h, a):
+            th[h, a] = new([P, 4, W], F32, f"th{h}{a}")
+            for t in range(4):
+                m = slice(t * P, (t + 1) * P)
+                for g in range(2):
+                    nc.tensor.matmul_mx(
+                        out=z[h, a, t][:],
+                        lhsT=wa_p[a][:, g, m].bitcast(FP8X4),
+                        lhsT_scale=ws_p[g][:, a, m],
+                        rhs=v_w[h][:, g, :].bitcast(FP4X4),
+                        rhs_scale=g_s0[h][:] if g == 0 else g_s1[h][:].bitcast(U8),
+                        start=False,
+                        stop=(g == 1),
+                    )
+                nc.scalar.activation(out=th[h, a][:, t, :], in_=z[h, a, t][:], func=ACT.Tanh)
+
+        def smooth(h, a):
+            hb[h, a] = new([P, 4 * W], BF16, f"hb{h}{a}")
+            nc.vector.tensor_tensor(
+                hb[h, a][:].rearrange("p (c i t) -> p c t i", t=4, i=4),
+                th[h, a][:].rearrange("p t (c i) -> p c t i", i=4),
+                sm_sb[:, a, :].unsqueeze(1).unsqueeze(3).to_broadcast([P, W // 4, 4, 4]),
+                ALU.mult,
+            )
+
+        def quantise(h, a):
+            hq[h, a] = new([P, W], U32, f"hq{h}{a}")
+            hs[h, a] = new([P, W], U8, f"hs{h}{a}")
+            nc.vector.quantize_mx(out=hq[h, a][:].bitcast(FP8X4), scales=hs[h, a][:], in_=hb[h, a][:])
+
+        def score(h):
+            accs = [psum.tile([P, W], F32, name="acc") for c in range(4)]
+            for a in range(2):
+                for c in range(4):
+                    nc.tensor.matmul_mx(
+                        out=accs[c][:],
+                        lhsT=en_w[:].bitcast(U8)[:, a, 2 * c * P : 2 * (c + 1) * P].bitcast(FP4X4),
+                        lhsT_scale=en_s[:].bitcast(U8)[:, a, c * P : (c + 1) * P],
+                        rhs=hq[h, a][:].bitcast(FP8X4),
+                        rhs_scale=hs[h, a][:],
+                        start=(a == 0),
+                        stop=(a == 1),
+                    )
+            for c in range(4):
+                y = new([P, W], F32, f"y{h}{c}")
+                if h == 1 and c % 2 == 1:
+                    nc.vector.tensor_scalar_add(y[:], accs[c][:], b_sb[:, c : c + 1])
+                else:
+                    nc.scalar.activation(out=y[:], in_=accs[c][:], func=ACT.Identity, bias=b_sb[:, c : c + 1])
+                nc.sync.dma_start(out[c * P : (c + 1) * P, h * W : (h + 1) * W], y[:])
+
+        gather2(0)
+        permute_scales()
+        permute_wb()
+        project2(0, 0)
+        project2(0, 1)
+        gather1(0)
+        permute_wa(0)
+        part(0)
+        project1(0, 0)
+        permute_wa(1)
+        project1(0, 1)
+        gather2(1)
+        project2(1, 0)
+        gather1(1)
+        part(1)
+        project1(1, 0)
+        project2(1, 1)
+        project1(1, 1)
+        smooth(0, 0)
+        smooth(0, 1)
+        quantise(0, 0)
+        quantise(0, 1)
+        smooth(1, 0)
+        score(0)
+        smooth(1, 1)
+        quantise(1, 0)
+        quantise(1, 1)
+        score(1)

@@ -29,70 +29,63 @@ def tile_list_kg_tanh_bias_kernel(
         keep = ctx.enter_context(tc.tile_pool(name="keep", bufs=1))
         psum = ctx.enter_context(tc.psum_pool(name="psum", bufs=8))
 
-        def new(shape, dtype, name):
-            return keep.tile(shape, dtype, name=name, align_bytes=64)
+        def new(shape, dtype, name, tag=None):
+            return keep.tile(shape, dtype, name=name, tag=tag or name, align_bytes=64)
 
         list1 = keep.tile([P, J // 16], U16, name="list1")
         list2 = keep.tile([P, J // 16], U16, name="list2")
+        warm_in = new([P, 1], F32, "warm_in", "tab2_w")
+        warm_out = new([P, 1], F32, "warm_out", "wb_w")
         tab_s = new([P, T // 4], I32, "tab_s")
         tab2_s = new([P, T // 4], I32, "tab2_s")
         w_s = new([P, R // 4], I32, "w_s")
-        en_s = new([P, 2, N // 4], I32, "en_s")
         tab_w = new([P, T], I32, "tab_w")
-        tab2_w = new([P, T], I32, "tab2_w")
-        wa_w = [new([P, 2, W], I32, f"wa_w{a}") for a in range(2)]
-        wb_w = new([P, R // 2], I32, "wb_w")
-        en_w = new([P, 2, N // 2], I32, "en_w")
+        wa_w = {0: new([P, 2, W], I32, "wa_w0")}
         sm_sb = new([P, 2, 4], F32, "sm_sb")
-        b_sb = new([P, 4], F32, "b_sb")
-        warm = new([P, 1], F32, "warm")
         g_s1 = [new([P, W // 4], I32, f"g_s1{h}") for h in range(2)]
 
-        nc.vector.memset(tab2_s[:], 0)
-        nc.vector.memset(w_s[:], 0)
+        nc.vector.memset(warm_in[:], 0.0)
         nc.vector.memset(tab_s[:], 0)
-        nc.vector.memset(warm[:], 0.0)
-        nc.scalar.activation(out=warm[:], in_=warm[:], func=ACT.Tanh)
+        nc.vector.memset(w_s[:], 0)
+        nc.gpsimd.memset(tab2_s[:], 0)
 
         wa_i = wa_words.rearrange("a p r i -> p a (r i)").bitcast(I32)
-        nc.sync.dma_start(list2[:], offs2)
         nc.sync.dma_start(list1[:], offs)
-        for q in range(4):
-            nc.sync.dma_start(tab2_s[32 * q : 32 * q + 4, :], tab2_scales[0, 4 * q : 4 * q + 4, :].bitcast(I32))
-        for q in range(4):
-            nc.sync.dma_start(w_s[32 * q : 32 * q + 4, :], wb_scales[0, 4 * q : 4 * q + 4, :].bitcast(I32))
-        for q in range(4):
-            nc.sync.dma_start(w_s[32 * q + 4 : 32 * q + 12, :], wa_scales[:, 4 * q : 4 * q + 4, :].bitcast(I32))
+        nc.scalar.dma_start(tab_w[:], tab_words[0].rearrange("p t i -> p (t i)").bitcast(I32))
+        nc.scalar.dma_start(wa_w[0][:], wa_i[:, :, 0:W])
+        nc.sync.dma_start(list2[:], offs2)
+        nc.scalar.activation(out=warm_out[:], in_=warm_in[:], func=ACT.Tanh)
         for q in range(4):
             nc.sync.dma_start(tab_s[32 * q : 32 * q + 8, :], tab_scales[:, 4 * q : 4 * q + 4, :].bitcast(I32))
-        nc.gpsimd.dma_start(tab2_w[:], tab2_words[0].rearrange("p t i -> p (t i)").bitcast(I32))
-        nc.gpsimd.dma_start(wb_w[:], wb_words[0].bitcast(I32))
-        nc.gpsimd.dma_start(tab_w[:], tab_words[0].rearrange("p t i -> p (t i)").bitcast(I32))
-        nc.gpsimd.dma_start(wa_w[0][:], wa_i[:, :, 0:W])
-        nc.gpsimd.dma_start(wa_w[1][:], wa_i[:, :, W : 2 * W])
-        nc.gpsimd.dma_start(sm_sb[:], sm.rearrange("(a p t) -> p a t", a=2, t=4))
-        nc.gpsimd.dma_start(en_w[:], en_words.rearrange("a p n -> p a n").bitcast(I32))
         for q in range(4):
-            nc.gpsimd.dma_start(
-                en_s[32 * q : 32 * q + 4, :, :],
-                en_scales[:, 4 * q : 4 * q + 4, :].rearrange("a r n -> r a n").bitcast(I32),
-            )
-        with nc.allow_non_contiguous_dma(reason="one bias value to a partition"):
-            nc.gpsimd.dma_start(b_sb[:], b.rearrange("(c p) -> p c", p=P))
+            nc.sync.dma_start(w_s[32 * q : 32 * q + 8, :], wa_scales[:, 4 * q : 4 * q + 4, :].bitcast(I32))
+        for q in range(4):
+            nc.sync.dma_start(w_s[32 * q + 8 : 32 * q + 12, :], wb_scales[0, 4 * q : 4 * q + 4, :].bitcast(I32))
+        tab2_w = new([P, T], I32, "tab2_w")
+        wb_w = new([P, R // 2], I32, "wb_w")
+        nc.scalar.dma_start(tab2_w[:], tab2_words[0].rearrange("p t i -> p (t i)").bitcast(I32))
+        for q in range(4):
+            nc.gpsimd.dma_start(tab2_s[32 * q : 32 * q + 4, :], tab2_scales[0, 4 * q : 4 * q + 4, :].bitcast(I32))
+        nc.scalar.dma_start(wb_w[:], wb_words[0].bitcast(I32))
+        nc.gpsimd.dma_start(sm_sb[:], sm.rearrange("(a p t) -> p a t", a=2, t=4))
 
-        g_s0 = [new([P, W], U8, f"g_s0{h}") for h in range(2)]
-        g_s2 = [new([P, W], U8, f"g_s2{h}") for h in range(2)]
-        g_w = [new([P, W], U32, f"g_w{h}") for h in range(2)]
-        g_w2 = [new([P, W], U32, f"g_w2{h}") for h in range(2)]
+        g_s0 = {}
+        g_s2 = {}
+        g_w = {}
+        g_w2 = {}
         v_w = [new([P, 2, 2 * W], U8, f"v_w{h}") for h in range(2)]
 
         def gather2(h):
             cols = slice(h * W // 16, (h + 1) * W // 16)
+            g_s2[h] = new([P, W], U8, f"g_s2{h}", "tab_w" if h == 1 else None)
+            g_w2[h] = new([P, W], U32, f"g_w2{h}", "tab_s" if h == 1 else None)
             nc.vector.tensor_copy(g_s2[h][:], tab2_s[:].bitcast(U8).indirect(list2[:, cols]))
             nc.vector.tensor_copy(g_w2[h][:], tab2_w[:].bitcast(U32).indirect(list2[:, cols]))
 
         def gather1(h):
             cols = slice(h * W // 16, (h + 1) * W // 16)
+            g_s0[h] = new([P, W], U8, f"g_s0{h}", "g_w0" if h == 1 else None)
+            g_w[h] = new([P, W], U32, f"g_w{h}", "wa_w0" if h == 1 else None)
             nc.vector.tensor_copy(g_s0[h][:], tab_s[:].bitcast(U8).indirect(list1[:, cols]))
             nc.sync.dma_start(g_s1[h][0:112, :], g_s0[h][4:116, :].bitcast(I32))
             nc.vector.tensor_copy(g_w[h][:], tab_w[:].bitcast(U32).indirect(list1[:, cols]))
@@ -102,17 +95,17 @@ def tile_list_kg_tanh_bias_kernel(
                 v_w[h][:].bitcast(U16), g_w[h][:].bitcast(U16).rearrange("p (j d) -> p d j", d=2)
             )
 
-        wa_p = [new([P, 2, W], I32, f"wa_p{a}") for a in range(2)]
+        wa_p = {}
         wb_p = new([P, 2, 2 * W], U8, "wb_p")
         ws_p = [new([P, 2, W], U8, f"ws_p{g}") for g in range(3)]
 
         def permute_scales():
             nc.vector.tensor_copy(
-                ws_p[2][:].rearrange("p a (t c i) -> p a c t i", t=4, i=16),
+                ws_p[0][:].rearrange("p a (t c i) -> p a c t i", t=4, i=16),
                 w_s[:].bitcast(U8).rearrange("p (a c i t) -> p a c t i", a=2, t=4, i=16),
             )
-            for g in range(2):
-                nc.sync.dma_start(ws_p[g][0:112].bitcast(I32), ws_p[2][4 + 4 * g : 116 + 4 * g].bitcast(I32))
+            for g in range(1, 3):
+                nc.sync.dma_start(ws_p[g][0:112].bitcast(I32), ws_p[0][4 * g : 112 + 4 * g].bitcast(I32))
 
         def permute_wb():
             nc.vector.tensor_copy(
@@ -121,6 +114,7 @@ def tile_list_kg_tanh_bias_kernel(
             )
 
         def permute_wa(a):
+            wa_p[a] = new([P, 2, W], I32, f"wa_p{a}")
             nc.vector.tensor_copy(
                 wa_p[a][:].rearrange("p g (t c i) -> p g c t i", t=4, i=4),
                 wa_w[a][:].rearrange("p g (c i t) -> p g c t i", t=4, i=4),
@@ -132,34 +126,35 @@ def tile_list_kg_tanh_bias_kernel(
         hs = {}
         z = {}
 
-        def project2(h, a):
-            for t in range(4):
+        def one_pass(h, a, t, g):
+            m = slice(t * P, (t + 1) * P)
+            if g == 0:
                 z[h, a, t] = psum.tile([P, W], F32, name="acc")
-                nc.tensor.matmul_mx(
-                    out=z[h, a, t][:],
-                    lhsT=wb_p[:, a, 2 * t * P : 2 * (t + 1) * P].bitcast(FP4X4),
-                    lhsT_scale=ws_p[2][:, a, t * P : (t + 1) * P],
-                    rhs=g_w2[h][:].bitcast(FP8X4),
-                    rhs_scale=g_s2[h][:],
-                    start=True,
-                    stop=False,
-                )
-
-        def project1(h, a):
-            th[h, a] = new([P, 4, W], F32, f"th{h}{a}")
-            for t in range(4):
-                m = slice(t * P, (t + 1) * P)
-                for g in range(2):
-                    nc.tensor.matmul_mx(
-                        out=z[h, a, t][:],
-                        lhsT=wa_p[a][:, g, m].bitcast(FP8X4),
-                        lhsT_scale=ws_p[g][:, a, m],
-                        rhs=v_w[h][:, g, :].bitcast(FP4X4),
-                        rhs_scale=g_s0[h][:] if g == 0 else g_s1[h][:].bitcast(U8),
-                        start=False,
-                        stop=(g == 1),
-                    )
+            if g < 2:
+                lhs = wa_p[a][:, g, m].bitcast(FP8X4)
+                rhs = v_w[h][:, g, :].bitcast(FP4X4)
+                rhs_scale = g_s0[h][:] if g == 0 else g_s1[h][:].bitcast(U8)
+            else:
+                lhs = wb_p[:, a, 2 * t * P : 2 * (t + 1) * P].bitcast(FP4X4)
+                rhs = g_w2[h][:].bitcast(FP8X4)
+                rhs_scale = g_s2[h][:]
+            nc.tensor.matmul_mx(
+                out=z[h, a, t][:],
+                lhsT=lhs,
+                lhsT_scale=ws_p[g][:, a, m],
+                rhs=rhs,
+                rhs_scale=rhs_scale,
+                start=(g == 0),
+                stop=(g == 2),
+            )
+            if g == 2:
                 nc.scalar.activation(out=th[h, a][:, t, :], in_=z[h, a, t][:], func=ACT.Tanh)
+
+        def project(h, a, by_pass):
+            th[h, a] = new([P, 4, W], F32, f"th{h}{a}")
+            order = [(t, g) for g in range(3) for t in range(4)] if by_pass else [(t, g) for t in range(4) for g in range(3)]
+            for t, g in order:
+                one_pass(h, a, t, g)
 
         def smooth(h, a):
             hb[h, a] = new([P, 4 * W], BF16, f"hb{h}{a}")
@@ -196,24 +191,33 @@ def tile_list_kg_tanh_bias_kernel(
                     nc.scalar.activation(out=y[:], in_=accs[c][:], func=ACT.Identity, bias=b_sb[:, c : c + 1])
                 nc.sync.dma_start(out[c * P : (c + 1) * P, h * W : (h + 1) * W], y[:])
 
-        gather2(0)
-        permute_scales()
-        permute_wb()
-        project2(0, 0)
-        project2(0, 1)
         gather1(0)
-        permute_wa(0)
         part(0)
-        project1(0, 0)
+        permute_scales()
+        wa_w[1] = new([P, 2, W], I32, "wa_w1", "w_s")
+        nc.scalar.dma_start(wa_w[1][:], wa_i[:, :, W : 2 * W])
+        permute_wa(0)
+        gather2(0)
+        permute_wb()
+        project(0, 0, True)
         permute_wa(1)
-        project1(0, 1)
-        gather2(1)
-        project2(1, 0)
+        en_w = new([P, 2, N // 2], I32, "en_w", "w_s")
+        nc.sync.dma_start(en_w[:], en_words.rearrange("a p n -> p a n").bitcast(I32))
+        en_s = new([P, 2, N // 4], I32, "en_s", "wb_w")
+        for q in range(4):
+            nc.sync.dma_start(
+                en_s[32 * q : 32 * q + 4, :, :],
+                en_scales[:, 4 * q : 4 * q + 4, :].rearrange("a r n -> r a n").bitcast(I32),
+            )
+        project(0, 1, False)
         gather1(1)
         part(1)
-        project1(1, 0)
-        project2(1, 1)
-        project1(1, 1)
+        b_sb = new([P, 4], F32, "b_sb", "wa_w0")
+        with nc.allow_non_contiguous_dma(reason="one bias value to a partition"):
+            nc.sync.dma_start(b_sb[:], b.rearrange("(c p) -> p c", p=P))
+        gather2(1)
+        project(1, 0, True)
+        project(1, 1, False)
         smooth(0, 0)
         smooth(0, 1)
         quantise(0, 0)

@@ -18,6 +18,12 @@ ALU = mybir.AluOpType
 
 P = 128
 W = 512
+PLACE = {
+    "wa_p0": 0, "w_s": 3584, "wa_p1": 4096,
+    "wa_w": 8192, "g_w20": 8192, "wb_p": 10240, "g_s2": 12288, "sm_sb": 13312,
+    "v_w1": 16384, "tab2_s": 18368, "g_s01": 18432, "g_w21": 18944,
+    "wb_w": 21504, "en_s": 21504, "en_w": 22528,
+}
 
 
 def tile_list_kg_tanh_bias_kernel(
@@ -27,33 +33,35 @@ def tile_list_kg_tanh_bias_kernel(
     nc = tc.nc
     with ExitStack() as ctx:
         keep = ctx.enter_context(tc.tile_pool(name="keep", bufs=1))
+        reuse = ctx.enter_context(tc.tile_pool(name="reuse", bufs=1))
         psum = ctx.enter_context(tc.psum_pool(name="psum", bufs=8))
 
         def new(shape, dtype, name, tag=None):
+            if name in PLACE:
+                return reuse.tile(shape, dtype, name=name, offset=PLACE[name], align_bytes=64)
             return keep.tile(shape, dtype, name=name, tag=tag or name, align_bytes=64)
 
         list1 = keep.tile([P, J // 16], U16, name="list1")
         list2 = keep.tile([P, J // 16], U16, name="list2")
-        warm_in = new([P, 1], F32, "warm_in", "tab2_w")
-        warm_out = new([P, 1], F32, "warm_out", "wb_w")
+        warm_in = new([P, 1], F32, "warm_in")
+        warm_out = new([P, 1], F32, "warm_out")
         tab_s = new([P, T // 4], I32, "tab_s")
         tab2_s = new([P, T // 4], I32, "tab2_s")
         w_s = new([P, R // 4], I32, "w_s")
         tab_w = new([P, T], I32, "tab_w")
-        wa_w = {0: new([P, 2, W], I32, "wa_w0")}
-        sm_sb = new([P, 2, 4], F32, "sm_sb")
+        wa_w = new([P, 2, R], I32, "wa_w")
         g_s1 = [new([P, W // 4], I32, f"g_s1{h}") for h in range(2)]
 
         nc.vector.memset(warm_in[:], 0.0)
         nc.vector.memset(tab_s[:], 0)
         nc.vector.memset(w_s[:], 0)
-        nc.gpsimd.memset(tab2_s[:], 0)
+        nc.vector.memset(tab2_s[:], 0)
 
         wa_i = wa_words.rearrange("a p r i -> p a (r i)").bitcast(I32)
         nc.sync.dma_start(list1[:], offs)
-        nc.scalar.dma_start(tab_w[:], tab_words[0].rearrange("p t i -> p (t i)").bitcast(I32))
-        nc.scalar.dma_start(wa_w[0][:], wa_i[:, :, 0:W])
         nc.sync.dma_start(list2[:], offs2)
+        nc.scalar.dma_start(tab_w[:], tab_words[0].rearrange("p t i -> p (t i)").bitcast(I32))
+        nc.gpsimd.dma_start(wa_w[:], wa_i)
         nc.scalar.activation(out=warm_out[:], in_=warm_in[:], func=ACT.Tanh)
         for q in range(4):
             nc.sync.dma_start(tab_s[32 * q : 32 * q + 8, :], tab_scales[:, 4 * q : 4 * q + 4, :].bitcast(I32))
@@ -61,42 +69,47 @@ def tile_list_kg_tanh_bias_kernel(
             nc.sync.dma_start(w_s[32 * q : 32 * q + 8, :], wa_scales[:, 4 * q : 4 * q + 4, :].bitcast(I32))
         for q in range(4):
             nc.sync.dma_start(w_s[32 * q + 8 : 32 * q + 12, :], wb_scales[0, 4 * q : 4 * q + 4, :].bitcast(I32))
+        for q in range(4):
+            nc.sync.dma_start(tab2_s[32 * q : 32 * q + 4, :], tab2_scales[0, 4 * q : 4 * q + 4, :].bitcast(I32))
         tab2_w = new([P, T], I32, "tab2_w")
         wb_w = new([P, R // 2], I32, "wb_w")
-        nc.scalar.dma_start(tab2_w[:], tab2_words[0].rearrange("p t i -> p (t i)").bitcast(I32))
-        for q in range(4):
-            nc.gpsimd.dma_start(tab2_s[32 * q : 32 * q + 4, :], tab2_scales[0, 4 * q : 4 * q + 4, :].bitcast(I32))
-        nc.scalar.dma_start(wb_w[:], wb_words[0].bitcast(I32))
-        nc.gpsimd.dma_start(sm_sb[:], sm.rearrange("(a p t) -> p a t", a=2, t=4))
+        nc.gpsimd.dma_start(tab2_w[:], tab2_words[0].rearrange("p t i -> p (t i)").bitcast(I32))
+        nc.gpsimd.dma_start(wb_w[:], wb_words[0].bitcast(I32))
 
         g_s0 = {}
         g_s2 = {}
         g_w = {}
         g_w2 = {}
-        v_w = [new([P, 2, 2 * W], U8, f"v_w{h}") for h in range(2)]
+        v_w = {}
 
-        def gather2(h):
+        def gather2_words(h):
             cols = slice(h * W // 16, (h + 1) * W // 16)
-            g_s2[h] = new([P, W], U8, f"g_s2{h}", "tab_w" if h == 1 else None)
-            g_w2[h] = new([P, W], U32, f"g_w2{h}", "tab_s" if h == 1 else None)
-            nc.vector.tensor_copy(g_s2[h][:], tab2_s[:].bitcast(U8).indirect(list2[:, cols]))
+            g_w2[h] = new([P, W], U32, f"g_w2{h}")
             nc.vector.tensor_copy(g_w2[h][:], tab2_w[:].bitcast(U32).indirect(list2[:, cols]))
 
-        def gather1(h):
+        def gather2_scales():
+            g_s2[0] = new([P, J], U8, "g_s2")
+            nc.vector.tensor_copy(g_s2[0][:], tab2_s[:].bitcast(U8).indirect(list2[:]))
+
+        def gather1_scales(h):
             cols = slice(h * W // 16, (h + 1) * W // 16)
-            g_s0[h] = new([P, W], U8, f"g_s0{h}", "g_w0" if h == 1 else None)
-            g_w[h] = new([P, W], U32, f"g_w{h}", "wa_w0" if h == 1 else None)
+            g_s0[h] = new([P, W], U8, f"g_s0{h}")
             nc.vector.tensor_copy(g_s0[h][:], tab_s[:].bitcast(U8).indirect(list1[:, cols]))
-            nc.sync.dma_start(g_s1[h][0:112, :], g_s0[h][4:116, :].bitcast(I32))
+            (nc.scalar if h == 0 else nc.sync).dma_start(g_s1[h][0:112, :], g_s0[h][4:116, :].bitcast(I32))
+
+        def gather1_words(h):
+            cols = slice(h * W // 16, (h + 1) * W // 16)
+            g_w[h] = new([P, W], U32, f"g_w{h}")
             nc.vector.tensor_copy(g_w[h][:], tab_w[:].bitcast(U32).indirect(list1[:, cols]))
 
         def part(h):
+            v_w[h] = new([P, 2, 2 * W], U8, f"v_w{h}")
             nc.vector.tensor_copy(
                 v_w[h][:].bitcast(U16), g_w[h][:].bitcast(U16).rearrange("p (j d) -> p d j", d=2)
             )
 
         wa_p = {}
-        wb_p = new([P, 2, 2 * W], U8, "wb_p")
+        wb_p = {}
         ws_p = [new([P, 2, W], U8, f"ws_p{g}") for g in range(3)]
 
         def permute_scales():
@@ -105,11 +118,12 @@ def tile_list_kg_tanh_bias_kernel(
                 w_s[:].bitcast(U8).rearrange("p (a c i t) -> p a c t i", a=2, t=4, i=16),
             )
             for g in range(1, 3):
-                nc.sync.dma_start(ws_p[g][0:112].bitcast(I32), ws_p[0][4 * g : 112 + 4 * g].bitcast(I32))
+                nc.scalar.dma_start(ws_p[g][0:112].bitcast(I32), ws_p[0][4 * g : 112 + 4 * g].bitcast(I32))
 
         def permute_wb():
+            wb_p[0] = new([P, 2, 2 * W], U8, "wb_p")
             nc.vector.tensor_copy(
-                wb_p[:].bitcast(U16).rearrange("p a (t c i) -> p a c t i", t=4, i=8),
+                wb_p[0][:].bitcast(U16).rearrange("p a (t c i) -> p a c t i", t=4, i=8),
                 wb_w[:].bitcast(U16).rearrange("p (a c i t) -> p a c t i", a=2, t=4, i=8),
             )
 
@@ -117,7 +131,7 @@ def tile_list_kg_tanh_bias_kernel(
             wa_p[a] = new([P, 2, W], I32, f"wa_p{a}")
             nc.vector.tensor_copy(
                 wa_p[a][:].rearrange("p g (t c i) -> p g c t i", t=4, i=4),
-                wa_w[a][:].rearrange("p g (c i t) -> p g c t i", t=4, i=4),
+                wa_w[:, :, a * W : (a + 1) * W].rearrange("p g (c i t) -> p g c t i", t=4, i=4),
             )
 
         th = {}
@@ -135,9 +149,9 @@ def tile_list_kg_tanh_bias_kernel(
                 rhs = v_w[h][:, g, :].bitcast(FP4X4)
                 rhs_scale = g_s0[h][:] if g == 0 else g_s1[h][:].bitcast(U8)
             else:
-                lhs = wb_p[:, a, 2 * t * P : 2 * (t + 1) * P].bitcast(FP4X4)
+                lhs = wb_p[0][:, a, 2 * t * P : 2 * (t + 1) * P].bitcast(FP4X4)
                 rhs = g_w2[h][:].bitcast(FP8X4)
-                rhs_scale = g_s2[h][:]
+                rhs_scale = g_s2[0][:, h * W : (h + 1) * W]
             nc.tensor.matmul_mx(
                 out=z[h, a, t][:],
                 lhsT=lhs,
@@ -150,9 +164,9 @@ def tile_list_kg_tanh_bias_kernel(
             if g == 2:
                 nc.scalar.activation(out=th[h, a][:, t, :], in_=z[h, a, t][:], func=ACT.Tanh)
 
-        def project(h, a, by_pass):
-            th[h, a] = new([P, 4, W], F32, f"th{h}{a}")
-            order = [(t, g) for g in range(3) for t in range(4)] if by_pass else [(t, g) for t in range(4) for g in range(3)]
+        def passes(h, a, order):
+            if (h, a) not in th:
+                th[h, a] = new([P, 4, W], F32, f"th{h}{a}")
             for t, g in order:
                 one_pass(h, a, t, g)
 
@@ -191,33 +205,38 @@ def tile_list_kg_tanh_bias_kernel(
                     nc.scalar.activation(out=y[:], in_=accs[c][:], func=ACT.Identity, bias=b_sb[:, c : c + 1])
                 nc.sync.dma_start(out[c * P : (c + 1) * P, h * W : (h + 1) * W], y[:])
 
-        gather1(0)
+        gather1_words(0)
+        gather1_scales(0)
         part(0)
+        gather1_words(1)
         permute_scales()
-        wa_w[1] = new([P, 2, W], I32, "wa_w1", "w_s")
-        nc.scalar.dma_start(wa_w[1][:], wa_i[:, :, W : 2 * W])
-        permute_wa(0)
-        gather2(0)
+        for a in range(2):
+            permute_wa(a)
+            passes(0, a, [(t, 0) for t in range(4)])
+        sm_sb = new([P, 2, 4], F32, "sm_sb")
+        nc.sync.dma_start(sm_sb[:], sm.rearrange("(a p t) -> p a t", a=2, t=4))
+        gather2_words(0)
         permute_wb()
-        project(0, 0, True)
-        permute_wa(1)
-        en_w = new([P, 2, N // 2], I32, "en_w", "w_s")
+        gather2_scales()
+        for g in range(1, 3):
+            for a in range(2):
+                passes(0, a, [(t, g) for t in range(4)])
+        en_s = new([P, 2, N // 4], I32, "en_s")
+        en_w = new([P, 2, N // 2], I32, "en_w")
         nc.sync.dma_start(en_w[:], en_words.rearrange("a p n -> p a n").bitcast(I32))
-        en_s = new([P, 2, N // 4], I32, "en_s", "wb_w")
         for q in range(4):
             nc.sync.dma_start(
                 en_s[32 * q : 32 * q + 4, :, :],
                 en_scales[:, 4 * q : 4 * q + 4, :].rearrange("a r n -> r a n").bitcast(I32),
             )
-        project(0, 1, False)
-        gather1(1)
+        gather1_scales(1)
         part(1)
-        b_sb = new([P, 4], F32, "b_sb", "wa_w0")
+        b_sb = new([P, 4], F32, "b_sb", "g_w1")
         with nc.allow_non_contiguous_dma(reason="one bias value to a partition"):
             nc.sync.dma_start(b_sb[:], b.rearrange("(c p) -> p c", p=P))
-        gather2(1)
-        project(1, 0, True)
-        project(1, 1, False)
+        gather2_words(1)
+        passes(1, 0, [(t, g) for g in range(3) for t in range(4)])
+        passes(1, 1, [(t, g) for t in range(4) for g in range(3)])
         smooth(0, 0)
         smooth(0, 1)
         quantise(0, 0)

@@ -20,9 +20,9 @@ P = 128
 W = 512
 PLACE = {
     "wa_p0": 0, "w_s": 3584, "wa_p1": 4096,
-    "wa_w": 8192, "g_w20": 8192, "wb_p": 10240, "g_s2": 12288, "sm_sb": 13312,
-    "v_w1": 16384, "tab2_s": 18368, "g_s01": 18432, "g_w21": 18944,
-    "wb_w": 21504, "en_s": 21504, "en_w": 22528,
+    "wa_w": 8192, "g_w20": 8192, "wb_p": 10240, "g_s2": 12288, "sm_sb": 13312, "g_s01": 13376,
+    "v_w1": 16384, "tab2_s": 18368, "g_w21": 18944,
+    "warm_out": 21504, "wb_w": 21504, "en_s": 21504, "en_w": 22528,
 }
 
 
@@ -43,7 +43,7 @@ def tile_list_kg_tanh_bias_kernel(
 
         list1 = keep.tile([P, J // 16], U16, name="list1")
         list2 = keep.tile([P, J // 16], U16, name="list2")
-        warm_in = new([P, 1], F32, "warm_in")
+        warm_in = new([P, 1], F32, "warm_in", "tab2_w")
         warm_out = new([P, 1], F32, "warm_out")
         tab_s = new([P, T // 4], I32, "tab_s")
         tab2_s = new([P, T // 4], I32, "tab2_s")
@@ -69,12 +69,12 @@ def tile_list_kg_tanh_bias_kernel(
             nc.sync.dma_start(w_s[32 * q : 32 * q + 8, :], wa_scales[:, 4 * q : 4 * q + 4, :].bitcast(I32))
         for q in range(4):
             nc.sync.dma_start(w_s[32 * q + 8 : 32 * q + 12, :], wb_scales[0, 4 * q : 4 * q + 4, :].bitcast(I32))
+        tab2_w = new([P, T], I32, "tab2_w")
+        nc.sync.dma_start(tab2_w[:], tab2_words[0].rearrange("p t i -> p (t i)").bitcast(I32))
         for q in range(4):
             nc.sync.dma_start(tab2_s[32 * q : 32 * q + 4, :], tab2_scales[0, 4 * q : 4 * q + 4, :].bitcast(I32))
-        tab2_w = new([P, T], I32, "tab2_w")
         wb_w = new([P, R // 2], I32, "wb_w")
-        nc.gpsimd.dma_start(tab2_w[:], tab2_words[0].rearrange("p t i -> p (t i)").bitcast(I32))
-        nc.gpsimd.dma_start(wb_w[:], wb_words[0].bitcast(I32))
+        nc.sync.dma_start(wb_w[:], wb_words[0].bitcast(I32))
 
         g_s0 = {}
         g_s2 = {}
@@ -215,6 +215,7 @@ def tile_list_kg_tanh_bias_kernel(
             passes(0, a, [(t, 0) for t in range(4)])
         sm_sb = new([P, 2, 4], F32, "sm_sb")
         nc.sync.dma_start(sm_sb[:], sm.rearrange("(a p t) -> p a t", a=2, t=4))
+        gather1_scales(1)
         gather2_words(0)
         permute_wb()
         gather2_scales()
@@ -229,13 +230,12 @@ def tile_list_kg_tanh_bias_kernel(
                 en_s[32 * q : 32 * q + 4, :, :],
                 en_scales[:, 4 * q : 4 * q + 4, :].rearrange("a r n -> r a n").bitcast(I32),
             )
-        gather1_scales(1)
         part(1)
         b_sb = new([P, 4], F32, "b_sb", "g_w1")
         with nc.allow_non_contiguous_dma(reason="one bias value to a partition"):
             nc.sync.dma_start(b_sb[:], b.rearrange("(c p) -> p c", p=P))
         gather2_words(1)
-        passes(1, 0, [(t, g) for g in range(3) for t in range(4)])
+        passes(1, 0, [(t, g) for t in range(4) for g in range(3)])
         passes(1, 1, [(t, g) for t in range(4) for g in range(3)])
         smooth(0, 0)
         smooth(0, 1)
@@ -243,7 +243,7 @@ def tile_list_kg_tanh_bias_kernel(
         quantise(0, 1)
         smooth(1, 0)
         score(0)
-        smooth(1, 1)
         quantise(1, 0)
+        smooth(1, 1)
         quantise(1, 1)
         score(1)

@@ -18,12 +18,7 @@ ALU = mybir.AluOpType
 
 P = 128
 W = 512
-PLACE = {
-    "wa_p0": 0, "w_s": 3584, "wa_p1": 4096,
-    "wa_w": 8192, "g_w20": 8192, "wb_p": 10240, "g_s2": 12288, "sm_sb": 13312, "g_s01": 13376,
-    "v_w1": 16384, "tab2_s": 18368, "g_w21": 18944,
-    "warm_out": 21504, "wb_w": 21504, "en_s": 21504, "en_w": 22528,
-}
+SHARE = {"g_w1": "wa_w0", "g_s21": "wb_w", "g_w21": "wa_w1"}
 
 
 def tile_list_kg_tanh_bias_kernel(
@@ -33,50 +28,56 @@ def tile_list_kg_tanh_bias_kernel(
     nc = tc.nc
     with ExitStack() as ctx:
         keep = ctx.enter_context(tc.tile_pool(name="keep", bufs=1))
-        reuse = ctx.enter_context(tc.tile_pool(name="reuse", bufs=1))
         psum = ctx.enter_context(tc.psum_pool(name="psum", bufs=8))
 
-        def new(shape, dtype, name, tag=None):
-            if name in PLACE:
-                return reuse.tile(shape, dtype, name=name, offset=PLACE[name], align_bytes=64)
-            return keep.tile(shape, dtype, name=name, tag=tag or name, align_bytes=64)
+        def new(shape, dtype, name):
+            return keep.tile(shape, dtype, name=name, tag=SHARE.get(name, name), align_bytes=64)
 
         list1 = keep.tile([P, J // 16], U16, name="list1")
         list2 = keep.tile([P, J // 16], U16, name="list2")
-        warm_in = new([P, 1], F32, "warm_in", "tab2_w")
+        warm_in = new([P, 1], F32, "warm_in")
         warm_out = new([P, 1], F32, "warm_out")
         tab_s = new([P, T // 4], I32, "tab_s")
         tab2_s = new([P, T // 4], I32, "tab2_s")
-        w_s = new([P, R // 4], I32, "w_s")
+        wa_s = new([P, 2, R // 4], I32, "wa_s")
+        wb_s = new([P, R // 4], I32, "wb_s")
         tab_w = new([P, T], I32, "tab_w")
-        wa_w = new([P, 2, R], I32, "wa_w")
-        g_s1 = [new([P, W // 4], I32, f"g_s1{h}") for h in range(2)]
+        tab2_w = new([P, T], I32, "tab2_w")
+        wa_w = {0: new([P, 2, W], I32, "wa_w0")}
+        wb_w = new([P, R // 2], I32, "wb_w")
+        v_s = [new([P, J // 4], I32, f"v_s{g}") for g in range(2)]
 
+        nc.vector.memset(wa_s[:], 0)
+        for q in range(4):
+            (nc.vector if q % 2 == 0 else nc.gpsimd).memset(tab_s[32 * q : 32 * q + 24, :], 0)
         nc.vector.memset(warm_in[:], 0.0)
-        nc.vector.memset(tab_s[:], 0)
-        nc.vector.memset(w_s[:], 0)
-        nc.vector.memset(tab2_s[:], 0)
+        nc.gpsimd.memset(tab2_s[:], 0)
+        nc.gpsimd.memset(wb_s[:], 0)
 
         wa_i = wa_words.rearrange("a p r i -> p a (r i)").bitcast(I32)
         nc.sync.dma_start(list1[:], offs)
         nc.sync.dma_start(list2[:], offs2)
-        nc.scalar.dma_start(tab_w[:], tab_words[0].rearrange("p t i -> p (t i)").bitcast(I32))
-        nc.gpsimd.dma_start(wa_w[:], wa_i)
+        for q in range(4):
+            nc.sync.dma_start(tab_s[32 * q + 24 : 32 * q + 32, :], tab_scales[:, 4 * q : 4 * q + 4, :].bitcast(I32))
+        nc.sync.dma_start(tab_w[:], tab_words[0].rearrange("p t i -> p (t i)").bitcast(I32))
+        nc.sync.dma_start(wa_w[0][:], wa_i[:, :, 0:W])
         nc.scalar.activation(out=warm_out[:], in_=warm_in[:], func=ACT.Tanh)
         for q in range(4):
-            nc.sync.dma_start(tab_s[32 * q : 32 * q + 8, :], tab_scales[:, 4 * q : 4 * q + 4, :].bitcast(I32))
-        for q in range(4):
-            nc.sync.dma_start(w_s[32 * q : 32 * q + 8, :], wa_scales[:, 4 * q : 4 * q + 4, :].bitcast(I32))
-        for q in range(4):
-            nc.sync.dma_start(w_s[32 * q + 8 : 32 * q + 12, :], wb_scales[0, 4 * q : 4 * q + 4, :].bitcast(I32))
-        tab2_w = new([P, T], I32, "tab2_w")
+            nc.sync.dma_start(
+                wa_s[32 * q : 32 * q + 4, :, :],
+                wa_scales[:, 4 * q : 4 * q + 4, :].rearrange("a r n -> r a n").bitcast(I32),
+            )
         nc.sync.dma_start(tab2_w[:], tab2_words[0].rearrange("p t i -> p (t i)").bitcast(I32))
         for q in range(4):
             nc.sync.dma_start(tab2_s[32 * q : 32 * q + 4, :], tab2_scales[0, 4 * q : 4 * q + 4, :].bitcast(I32))
-        wb_w = new([P, R // 2], I32, "wb_w")
         nc.sync.dma_start(wb_w[:], wb_words[0].bitcast(I32))
+        for q in range(4):
+            nc.sync.dma_start(wb_s[32 * q : 32 * q + 4, :], wb_scales[0, 4 * q : 4 * q + 4, :].bitcast(I32))
+        wa_w[1] = new([P, 2, W], I32, "wa_w1")
+        nc.sync.dma_start(wa_w[1][:], wa_i[:, :, W : 2 * W])
+        sm_sb = new([P, 2, 4], F32, "sm_sb")
+        nc.sync.dma_start(sm_sb[:], sm.rearrange("(a p t) -> p a t", a=2, t=4))
 
-        g_s0 = {}
         g_s2 = {}
         g_w = {}
         g_w2 = {}
@@ -87,15 +88,16 @@ def tile_list_kg_tanh_bias_kernel(
             g_w2[h] = new([P, W], U32, f"g_w2{h}")
             nc.vector.tensor_copy(g_w2[h][:], tab2_w[:].bitcast(U32).indirect(list2[:, cols]))
 
-        def gather2_scales():
-            g_s2[0] = new([P, J], U8, "g_s2")
-            nc.vector.tensor_copy(g_s2[0][:], tab2_s[:].bitcast(U8).indirect(list2[:]))
-
-        def gather1_scales(h):
+        def gather2_scales(h):
             cols = slice(h * W // 16, (h + 1) * W // 16)
-            g_s0[h] = new([P, W], U8, f"g_s0{h}")
-            nc.vector.tensor_copy(g_s0[h][:], tab_s[:].bitcast(U8).indirect(list1[:, cols]))
-            (nc.scalar if h == 0 else nc.sync).dma_start(g_s1[h][0:112, :], g_s0[h][4:116, :].bitcast(I32))
+            g_s2[h] = new([P, W], U8, f"g_s2{h}")
+            nc.vector.tensor_copy(g_s2[h][:], tab2_s[:].bitcast(U8).indirect(list2[:, cols]))
+
+        def gather1_scales():
+            g_s = new([P, J], U8, "g_s")
+            nc.vector.tensor_copy(g_s[:], tab_s[:].bitcast(U8).indirect(list1[:]))
+            for g in range(2):
+                nc.scalar.dma_start(v_s[g][0:100, :], g_s[24 + 4 * g : 124 + 4 * g, :].bitcast(I32))
 
         def gather1_words(h):
             cols = slice(h * W // 16, (h + 1) * W // 16)
@@ -112,13 +114,11 @@ def tile_list_kg_tanh_bias_kernel(
         wb_p = {}
         ws_p = [new([P, 2, W], U8, f"ws_p{g}") for g in range(3)]
 
-        def permute_scales():
-            nc.vector.tensor_copy(
-                ws_p[0][:].rearrange("p a (t c i) -> p a c t i", t=4, i=16),
-                w_s[:].bitcast(U8).rearrange("p (a c i t) -> p a c t i", a=2, t=4, i=16),
+        def permute_scales(dst, src):
+            nc.gpsimd.tensor_copy(
+                dst[:].rearrange("p a (t c i) -> p a c t i", t=4, i=16),
+                src.bitcast(U8).rearrange("p (a c i t) -> p a c t i", a=2, t=4, i=16),
             )
-            for g in range(1, 3):
-                nc.scalar.dma_start(ws_p[g][0:112].bitcast(I32), ws_p[0][4 * g : 112 + 4 * g].bitcast(I32))
 
         def permute_wb():
             wb_p[0] = new([P, 2, 2 * W], U8, "wb_p")
@@ -131,7 +131,7 @@ def tile_list_kg_tanh_bias_kernel(
             wa_p[a] = new([P, 2, W], I32, f"wa_p{a}")
             nc.vector.tensor_copy(
                 wa_p[a][:].rearrange("p g (t c i) -> p g c t i", t=4, i=4),
-                wa_w[:, :, a * W : (a + 1) * W].rearrange("p g (c i t) -> p g c t i", t=4, i=4),
+                wa_w[a][:].rearrange("p g (c i t) -> p g c t i", t=4, i=4),
             )
 
         th = {}
@@ -147,11 +147,11 @@ def tile_list_kg_tanh_bias_kernel(
             if g < 2:
                 lhs = wa_p[a][:, g, m].bitcast(FP8X4)
                 rhs = v_w[h][:, g, :].bitcast(FP4X4)
-                rhs_scale = g_s0[h][:] if g == 0 else g_s1[h][:].bitcast(U8)
+                rhs_scale = v_s[g][:].bitcast(U8)[:, h * W : (h + 1) * W]
             else:
                 lhs = wb_p[0][:, a, 2 * t * P : 2 * (t + 1) * P].bitcast(FP4X4)
                 rhs = g_w2[h][:].bitcast(FP8X4)
-                rhs_scale = g_s2[0][:, h * W : (h + 1) * W]
+                rhs_scale = g_s2[h][:]
             nc.tensor.matmul_mx(
                 out=z[h, a, t][:],
                 lhsT=lhs,
@@ -205,23 +205,26 @@ def tile_list_kg_tanh_bias_kernel(
                     nc.scalar.activation(out=y[:], in_=accs[c][:], func=ACT.Identity, bias=b_sb[:, c : c + 1])
                 nc.sync.dma_start(out[c * P : (c + 1) * P, h * W : (h + 1) * W], y[:])
 
+        gather1_scales()
         gather1_words(0)
-        gather1_scales(0)
         part(0)
+        permute_wa(0)
+        for g in range(2):
+            permute_scales(ws_p[g], wa_s[:, g, :])
+        permute_scales(ws_p[2], wb_s[:])
         gather1_words(1)
-        permute_scales()
-        for a in range(2):
-            permute_wa(a)
-            passes(0, a, [(t, 0) for t in range(4)])
-        sm_sb = new([P, 2, 4], F32, "sm_sb")
-        nc.sync.dma_start(sm_sb[:], sm.rearrange("(a p t) -> p a t", a=2, t=4))
-        gather1_scales(1)
+        part(1)
+        for g in range(2):
+            for h in range(2):
+                passes(h, 0, [(t, g) for t in range(4)])
         gather2_words(0)
+        gather2_scales(0)
         permute_wb()
-        gather2_scales()
-        for g in range(1, 3):
-            for a in range(2):
-                passes(0, a, [(t, g) for t in range(4)])
+        passes(0, 0, [(t, 2) for t in range(4)])
+        gather2_scales(1)
+        permute_wa(1)
+        passes(0, 1, [(t, g) for t in range(4) for g in range(3)])
+        gather2_words(1)
         en_s = new([P, 2, N // 4], I32, "en_s")
         en_w = new([P, 2, N // 2], I32, "en_w")
         nc.sync.dma_start(en_w[:], en_words.rearrange("a p n -> p a n").bitcast(I32))
@@ -230,12 +233,10 @@ def tile_list_kg_tanh_bias_kernel(
                 en_s[32 * q : 32 * q + 4, :, :],
                 en_scales[:, 4 * q : 4 * q + 4, :].rearrange("a r n -> r a n").bitcast(I32),
             )
-        part(1)
-        b_sb = new([P, 4], F32, "b_sb", "g_w1")
+        b_sb = new([P, 4], F32, "b_sb")
         with nc.allow_non_contiguous_dma(reason="one bias value to a partition"):
             nc.sync.dma_start(b_sb[:], b.rearrange("(c p) -> p c", p=P))
-        gather2_words(1)
-        passes(1, 0, [(t, g) for t in range(4) for g in range(3)])
+        passes(1, 0, [(t, 2) for t in range(4)])
         passes(1, 1, [(t, g) for t in range(4) for g in range(3)])
         smooth(0, 0)
         smooth(0, 1)

@@ -173,9 +173,9 @@ def tile_list_kg_tanh_bias_kernel(
         def smooth(h, a):
             hb[h, a] = new([P, 4 * W], BF16, f"hb{h}{a}")
             nc.vector.tensor_tensor(
-                hb[h, a][:].rearrange("p (c i t) -> p c t i", t=4, i=4),
-                th[h, a][:].rearrange("p t (c i) -> p c t i", i=4),
-                sm_sb[:, a, :].unsqueeze(1).unsqueeze(3).to_broadcast([P, W // 4, 4, 4]),
+                hb[h, a][:].rearrange("p (c i t) -> p c t i", t=4, i=2),
+                th[h, a][:].rearrange("p t (c i) -> p c t i", i=2),
+                sm_sb[:, a, :].unsqueeze(1).unsqueeze(3).to_broadcast([P, W // 2, 4, 2]),
                 ALU.mult,
             )
 

@@ -1,6 +1,7 @@
 from contextlib import ExitStack
 
 import concourse.mybir as mybir
+from concourse.masks import make_identity
 
 K, L, R, N, T, J = 1024, 512, 1024, 512, 2048, 1024
 FLOPS = 2 * J * R * (K + L + N)
@@ -18,7 +19,12 @@ ALU = mybir.AluOpType
 
 P = 128
 W = 512
-SHARE = {"g_w1": "wa_w0", "g_s21": "wb_w", "g_w21": "wa_w1"}
+SPLIT = 368
+PLACE = {
+    "wa_w0": 0, "g_w1": 0, "g_s20": 0,
+    "wa_w1": 4096, "g_w21": 4096, "g_s21": 6144,
+    "v_s0": 8192, "sm_pad": 8960, "v_s1": 9216,
+}
 
 
 def tile_list_kg_tanh_bias_kernel(
@@ -28,10 +34,16 @@ def tile_list_kg_tanh_bias_kernel(
     nc = tc.nc
     with ExitStack() as ctx:
         keep = ctx.enter_context(tc.tile_pool(name="keep", bufs=1))
-        psum = ctx.enter_context(tc.psum_pool(name="psum", bufs=8))
+        reuse = ctx.enter_context(tc.tile_pool(name="reuse", bufs=1))
+        psum = ctx.enter_context(tc.psum_pool(name="psum", bufs=1))
 
         def new(shape, dtype, name):
-            return keep.tile(shape, dtype, name=name, tag=SHARE.get(name, name), align_bytes=64)
+            if name in PLACE:
+                return reuse.tile(shape, dtype, name=name, offset=PLACE[name], align_bytes=64)
+            return keep.tile(shape, dtype, name=name, align_bytes=64)
+
+        def bank(i):
+            return psum.tile([P, W], F32, name=f"bank{i}")
 
         list1 = keep.tile([P, J // 16], U16, name="list1")
         list2 = keep.tile([P, J // 16], U16, name="list2")
@@ -45,7 +57,6 @@ def tile_list_kg_tanh_bias_kernel(
         tab2_w = new([P, T], I32, "tab2_w")
         wa_w = {0: new([P, 2, W], I32, "wa_w0")}
         wb_w = new([P, R // 2], I32, "wb_w")
-        v_s = [new([P, J // 4], I32, f"v_s{g}") for g in range(2)]
 
         nc.vector.memset(wa_s[:], 0)
         for q in range(4):
@@ -53,13 +64,17 @@ def tile_list_kg_tanh_bias_kernel(
         nc.vector.memset(warm_in[:], 0.0)
         nc.gpsimd.memset(tab2_s[:], 0)
         nc.gpsimd.memset(wb_s[:], 0)
+        ident = new([P, P], F32, "ident")
+        make_identity(nc, ident[:])
+        sm_pad = new([P, P], F32, "sm_pad")
+        nc.vector.memset(sm_pad[:, 8:P], 0.0)
 
         wa_i = wa_words.rearrange("a p r i -> p a (r i)").bitcast(I32)
         nc.sync.dma_start(list1[:], offs)
-        nc.sync.dma_start(list2[:], offs2)
         for q in range(4):
             nc.sync.dma_start(tab_s[32 * q + 24 : 32 * q + 32, :], tab_scales[:, 4 * q : 4 * q + 4, :].bitcast(I32))
         nc.sync.dma_start(tab_w[:], tab_words[0].rearrange("p t i -> p (t i)").bitcast(I32))
+        nc.sync.dma_start(sm_pad[:, 0:8].rearrange("p (a t) -> p a t", a=2), sm.rearrange("(a p t) -> p a t", a=2, t=4))
         nc.sync.dma_start(wa_w[0][:], wa_i[:, :, 0:W])
         nc.scalar.activation(out=warm_out[:], in_=warm_in[:], func=ACT.Tanh)
         for q in range(4):
@@ -68,6 +83,7 @@ def tile_list_kg_tanh_bias_kernel(
                 wa_scales[:, 4 * q : 4 * q + 4, :].rearrange("a r n -> r a n").bitcast(I32),
             )
         nc.sync.dma_start(tab2_w[:], tab2_words[0].rearrange("p t i -> p (t i)").bitcast(I32))
+        nc.sync.dma_start(list2[:], offs2)
         for q in range(4):
             nc.sync.dma_start(tab2_s[32 * q : 32 * q + 4, :], tab2_scales[0, 4 * q : 4 * q + 4, :].bitcast(I32))
         nc.sync.dma_start(wb_w[:], wb_words[0].bitcast(I32))
@@ -75,9 +91,17 @@ def tile_list_kg_tanh_bias_kernel(
             nc.sync.dma_start(wb_s[32 * q : 32 * q + 4, :], wb_scales[0, 4 * q : 4 * q + 4, :].bitcast(I32))
         wa_w[1] = new([P, 2, W], I32, "wa_w1")
         nc.sync.dma_start(wa_w[1][:], wa_i[:, :, W : 2 * W])
-        sm_sb = new([P, 2, 4], F32, "sm_sb")
-        nc.sync.dma_start(sm_sb[:], sm.rearrange("(a p t) -> p a t", a=2, t=4))
 
+        sm_ps = psum.tile([P, 2, P], F32, name="sm_ps")
+        sm_t = new([P, P], F32, "sm_t")
+        nc.tensor.transpose(sm_ps[:, 0, :], sm_pad[:], ident[:])
+        nc.scalar.copy(sm_t[:], sm_ps[:, 0, :])
+        nc.tensor.transpose(sm_ps[:, 1, :], sm_t[:], ident[:])
+        sm_sb = new([P, 2, 4], F32, "sm_sb")
+        nc.scalar.copy(sm_sb[:].rearrange("p a t -> p (a t)"), sm_ps[:, 1, 0:8])
+        v_s = [new([P, J // 4], I32, f"v_s{g}") for g in range(2)]
+
+        g_s = new([P, J], U8, "g_s")
         g_s2 = {}
         g_w = {}
         g_w2 = {}
@@ -94,7 +118,6 @@ def tile_list_kg_tanh_bias_kernel(
             nc.vector.tensor_copy(g_s2[h][:], tab2_s[:].bitcast(U8).indirect(list2[:, cols]))
 
         def gather1_scales():
-            g_s = new([P, J], U8, "g_s")
             nc.vector.tensor_copy(g_s[:], tab_s[:].bitcast(U8).indirect(list1[:]))
             for g in range(2):
                 nc.scalar.dma_start(v_s[g][0:100, :], g_s[24 + 4 * g : 124 + 4 * g, :].bitcast(I32))
@@ -112,12 +135,12 @@ def tile_list_kg_tanh_bias_kernel(
 
         wa_p = {}
         wb_p = {}
-        ws_p = [new([P, 2, W], U8, f"ws_p{g}") for g in range(3)]
+        ws_p = {(g, a): new([P, W], U8, f"ws_p{g}{a}") for g in range(3) for a in range(2)}
 
-        def permute_scales(dst, src):
+        def permute_scales(g, a, src):
             nc.gpsimd.tensor_copy(
-                dst[:].rearrange("p a (t c i) -> p a c t i", t=4, i=16),
-                src.bitcast(U8).rearrange("p (a c i t) -> p a c t i", a=2, t=4, i=16),
+                ws_p[g, a][:].rearrange("p (t c i) -> p c t i", t=4, i=16),
+                src.bitcast(U8)[:, a * W : (a + 1) * W].rearrange("p (c i t) -> p c t i", t=4, i=16),
             )
 
         def permute_wb():
@@ -143,7 +166,7 @@ def tile_list_kg_tanh_bias_kernel(
         def one_pass(h, a, t, g):
             m = slice(t * P, (t + 1) * P)
             if g == 0:
-                z[h, a, t] = psum.tile([P, W], F32, name="acc")
+                z[h, a, t] = bank(4 + t % 3 if (h, a) == (1, 0) else t)
             if g < 2:
                 lhs = wa_p[a][:, g, m].bitcast(FP8X4)
                 rhs = v_w[h][:, g, :].bitcast(FP4X4)
@@ -155,7 +178,7 @@ def tile_list_kg_tanh_bias_kernel(
             nc.tensor.matmul_mx(
                 out=z[h, a, t][:],
                 lhsT=lhs,
-                lhsT_scale=ws_p[g][:, a, m],
+                lhsT_scale=ws_p[g, a][:, m],
                 rhs=rhs,
                 rhs_scale=rhs_scale,
                 start=(g == 0),
@@ -173,9 +196,15 @@ def tile_list_kg_tanh_bias_kernel(
         def smooth(h, a):
             hb[h, a] = new([P, 4 * W], BF16, f"hb{h}{a}")
             nc.vector.tensor_tensor(
-                hb[h, a][:].rearrange("p (c i t) -> p c t i", t=4, i=2),
-                th[h, a][:].rearrange("p t (c i) -> p c t i", i=2),
-                sm_sb[:, a, :].unsqueeze(1).unsqueeze(3).to_broadcast([P, W // 2, 4, 2]),
+                hb[h, a][:, 0 : 4 * SPLIT].rearrange("p (c i t) -> p c t i", t=4, i=2),
+                th[h, a][:, :, 0:SPLIT].rearrange("p t (c i) -> p c t i", i=2),
+                sm_ps[:, 1, 4 * a : 4 * a + 4].unsqueeze(1).unsqueeze(3).to_broadcast([P, SPLIT // 2, 4, 2]),
+                ALU.mult,
+            )
+            nc.gpsimd.tensor_tensor(
+                hb[h, a][:, 4 * SPLIT : 4 * W].rearrange("p (j t) -> p j t", t=4),
+                th[h, a][:, :, SPLIT:W].rearrange("p t j -> p j t"),
+                sm_sb[:, a, :].unsqueeze(1).to_broadcast([P, W - SPLIT, 4]),
                 ALU.mult,
             )
 
@@ -185,7 +214,7 @@ def tile_list_kg_tanh_bias_kernel(
             nc.vector.quantize_mx(out=hq[h, a][:].bitcast(FP8X4), scales=hs[h, a][:], in_=hb[h, a][:])
 
         def score(h):
-            accs = [psum.tile([P, W], F32, name="acc") for c in range(4)]
+            accs = [bank(c if h == 0 else (4 + c if c < 3 else 0)) for c in range(4)]
             for a in range(2):
                 for c in range(4):
                     nc.tensor.matmul_mx(
@@ -209,21 +238,34 @@ def tile_list_kg_tanh_bias_kernel(
         gather1_words(0)
         part(0)
         permute_wa(0)
-        for g in range(2):
-            permute_scales(ws_p[g], wa_s[:, g, :])
-        permute_scales(ws_p[2], wb_s[:])
+        warm_acc = bank(4)
+        for i in range(3):
+            nc.tensor.matmul_mx(
+                out=warm_acc[:],
+                lhsT=wa_p[0][:, 0, 0:P].bitcast(FP8X4),
+                lhsT_scale=wa_s[:, 0, :].bitcast(U8)[:, 0:P],
+                rhs=v_w[0][:, 0, :].bitcast(FP4X4),
+                rhs_scale=g_s[:, 0:W],
+                start=True,
+                stop=True,
+            )
+        for a in range(2):
+            for g in range(2):
+                permute_scales(g, a, wa_s[:, g, :])
+        for a in range(2):
+            permute_scales(2, a, wb_s[:])
         gather1_words(1)
         part(1)
         for g in range(2):
             for h in range(2):
-                passes(h, 0, [(t, g) for t in range(4)])
-        gather2_words(0)
+                passes(h, 0, [(t, g) for t in range(4 - h)])
         gather2_scales(0)
+        gather2_words(0)
         permute_wb()
         passes(0, 0, [(t, 2) for t in range(4)])
-        gather2_scales(1)
         permute_wa(1)
         passes(0, 1, [(t, g) for t in range(4) for g in range(3)])
+        gather2_scales(1)
         gather2_words(1)
         en_s = new([P, 2, N // 4], I32, "en_s")
         en_w = new([P, 2, N // 2], I32, "en_w")
@@ -236,7 +278,7 @@ def tile_list_kg_tanh_bias_kernel(
         b_sb = new([P, 4], F32, "b_sb")
         with nc.allow_non_contiguous_dma(reason="one bias value to a partition"):
             nc.sync.dma_start(b_sb[:], b.rearrange("(c p) -> p c", p=P))
-        passes(1, 0, [(t, 2) for t in range(4)])
+        passes(1, 0, [(t, 2) for t in range(3)] + [(3, g) for g in range(3)])
         passes(1, 1, [(t, g) for t in range(4) for g in range(3)])
         smooth(0, 0)
         smooth(0, 1)

@@ -1,7 +1,6 @@
 from contextlib import ExitStack
 
 import concourse.mybir as mybir
-from concourse.masks import make_identity
 
 K, L, R, N, T, J = 1024, 512, 1024, 512, 2048, 1024
 FLOPS = 2 * J * R * (K + L + N)
@@ -19,11 +18,11 @@ ALU = mybir.AluOpType
 
 P = 128
 W = 512
-SPLIT = 368
 PLACE = {
-    "wa_w0": 0, "g_w1": 0, "g_s20": 0,
-    "wa_w1": 4096, "g_w21": 4096, "g_s21": 6144,
-    "v_s0": 8192, "sm_pad": 8960, "v_s1": 9216,
+    "tab_w": 16384, "g_s20": 16384,
+    "wb_w": 4096, "g_s21": 4096, "g_w21": 5120,
+    "wa_w1": 10240, "v_w11": 10240,
+    "v_s0": 8192, "warm_out": 9152, "v_s1": 9216,
 }
 
 
@@ -47,8 +46,8 @@ def tile_list_kg_tanh_bias_kernel(
 
         list1 = keep.tile([P, J // 16], U16, name="list1")
         list2 = keep.tile([P, J // 16], U16, name="list2")
-        warm_in = new([P, 1], F32, "warm_in")
-        warm_out = new([P, 1], F32, "warm_out")
+        sm_sb = new([P, 2, 4], F32, "sm_sb")
+        warm_out = new([P, 32], F32, "warm_out")
         tab_s = new([P, T // 4], I32, "tab_s")
         tab2_s = new([P, T // 4], I32, "tab2_s")
         wa_s = new([P, 2, R // 4], I32, "wa_s")
@@ -61,22 +60,17 @@ def tile_list_kg_tanh_bias_kernel(
         nc.vector.memset(wa_s[:], 0)
         for q in range(4):
             (nc.vector if q % 2 == 0 else nc.gpsimd).memset(tab_s[32 * q : 32 * q + 24, :], 0)
-        nc.vector.memset(warm_in[:], 0.0)
         nc.gpsimd.memset(tab2_s[:], 0)
         nc.gpsimd.memset(wb_s[:], 0)
-        ident = new([P, P], F32, "ident")
-        make_identity(nc, ident[:])
-        sm_pad = new([P, P], F32, "sm_pad")
-        nc.vector.memset(sm_pad[:, 8:P], 0.0)
 
         wa_i = wa_words.rearrange("a p r i -> p a (r i)").bitcast(I32)
         nc.sync.dma_start(list1[:], offs)
         for q in range(4):
             nc.sync.dma_start(tab_s[32 * q + 24 : 32 * q + 32, :], tab_scales[:, 4 * q : 4 * q + 4, :].bitcast(I32))
         nc.sync.dma_start(tab_w[:], tab_words[0].rearrange("p t i -> p (t i)").bitcast(I32))
-        nc.sync.dma_start(sm_pad[:, 0:8].rearrange("p (a t) -> p a t", a=2), sm.rearrange("(a p t) -> p a t", a=2, t=4))
+        nc.sync.dma_start(sm_sb[:], sm.rearrange("(a p t) -> p a t", a=2, t=4))
         nc.sync.dma_start(wa_w[0][:], wa_i[:, :, 0:W])
-        nc.scalar.activation(out=warm_out[:], in_=warm_in[:], func=ACT.Tanh)
+        nc.scalar.activation(out=warm_out[:, 0:1], in_=sm_sb[:, 0, 0:1], func=ACT.Tanh)
         for q in range(4):
             nc.sync.dma_start(
                 wa_s[32 * q : 32 * q + 4, :, :],
@@ -92,13 +86,6 @@ def tile_list_kg_tanh_bias_kernel(
         wa_w[1] = new([P, 2, W], I32, "wa_w1")
         nc.sync.dma_start(wa_w[1][:], wa_i[:, :, W : 2 * W])
 
-        sm_ps = psum.tile([P, 2, P], F32, name="sm_ps")
-        sm_t = new([P, P], F32, "sm_t")
-        nc.tensor.transpose(sm_ps[:, 0, :], sm_pad[:], ident[:])
-        nc.scalar.copy(sm_t[:], sm_ps[:, 0, :])
-        nc.tensor.transpose(sm_ps[:, 1, :], sm_t[:], ident[:])
-        sm_sb = new([P, 2, 4], F32, "sm_sb")
-        nc.scalar.copy(sm_sb[:].rearrange("p a t -> p (a t)"), sm_ps[:, 1, 0:8])
         v_s = [new([P, J // 4], I32, f"v_s{g}") for g in range(2)]
 
         g_s = new([P, J], U8, "g_s")
@@ -127,11 +114,16 @@ def tile_list_kg_tanh_bias_kernel(
             g_w[h] = new([P, W], U32, f"g_w{h}")
             nc.vector.tensor_copy(g_w[h][:], tab_w[:].bitcast(U32).indirect(list1[:, cols]))
 
-        def part(h):
-            v_w[h] = new([P, 2, 2 * W], U8, f"v_w{h}")
-            nc.vector.tensor_copy(
-                v_w[h][:].bitcast(U16), g_w[h][:].bitcast(U16).rearrange("p (j d) -> p d j", d=2)
-            )
+        def part_both(h):
+            both = new([P, 2, 2 * W], U8, f"v_w{h}")
+            nc.vector.tensor_copy(both[:].bitcast(U16), g_w[h][:].bitcast(U16).rearrange("p (j d) -> p d j", d=2))
+            v_w[h, 0] = both[:, 0, :]
+            v_w[h, 1] = both[:, 1, :]
+
+        def part(h, d):
+            one = new([P, 2 * W], U8, f"v_w{h}{d}")
+            nc.vector.tensor_copy(one[:].bitcast(U16), g_w[h][:].bitcast(U16).rearrange("p (j d) -> p d j", d=2)[:, d, :])
+            v_w[h, d] = one[:]
 
         wa_p = {}
         wb_p = {}
@@ -152,7 +144,7 @@ def tile_list_kg_tanh_bias_kernel(
 
         def permute_wa(a):
             wa_p[a] = new([P, 2, W], I32, f"wa_p{a}")
-            nc.vector.tensor_copy(
+            nc.gpsimd.tensor_copy(
                 wa_p[a][:].rearrange("p g (t c i) -> p g c t i", t=4, i=4),
                 wa_w[a][:].rearrange("p g (c i t) -> p g c t i", t=4, i=4),
             )
@@ -166,10 +158,10 @@ def tile_list_kg_tanh_bias_kernel(
         def one_pass(h, a, t, g):
             m = slice(t * P, (t + 1) * P)
             if g == 0:
-                z[h, a, t] = bank(4 + t % 3 if (h, a) == (1, 0) else t)
+                z[h, a, t] = bank(4 + t if (h, a) == (1, 0) else t)
             if g < 2:
                 lhs = wa_p[a][:, g, m].bitcast(FP8X4)
-                rhs = v_w[h][:, g, :].bitcast(FP4X4)
+                rhs = v_w[h, g].bitcast(FP4X4)
                 rhs_scale = v_s[g][:].bitcast(U8)[:, h * W : (h + 1) * W]
             else:
                 lhs = wb_p[0][:, a, 2 * t * P : 2 * (t + 1) * P].bitcast(FP4X4)
@@ -193,72 +185,77 @@ def tile_list_kg_tanh_bias_kernel(
             for t, g in order:
                 one_pass(h, a, t, g)
 
-        def smooth(h, a):
-            hb[h, a] = new([P, 4 * W], BF16, f"hb{h}{a}")
+        def smooth(h, a, j0=0, width=W):
+            if (h, a) not in hb:
+                hb[h, a] = new([P, 4 * W], BF16, f"hb{h}{a}")
             nc.vector.tensor_tensor(
-                hb[h, a][:, 0 : 4 * SPLIT].rearrange("p (c i t) -> p c t i", t=4, i=2),
-                th[h, a][:, :, 0:SPLIT].rearrange("p t (c i) -> p c t i", i=2),
-                sm_ps[:, 1, 4 * a : 4 * a + 4].unsqueeze(1).unsqueeze(3).to_broadcast([P, SPLIT // 2, 4, 2]),
-                ALU.mult,
-            )
-            nc.gpsimd.tensor_tensor(
-                hb[h, a][:, 4 * SPLIT : 4 * W].rearrange("p (j t) -> p j t", t=4),
-                th[h, a][:, :, SPLIT:W].rearrange("p t j -> p j t"),
-                sm_sb[:, a, :].unsqueeze(1).to_broadcast([P, W - SPLIT, 4]),
+                hb[h, a][:, 4 * j0 : 4 * (j0 + width)].rearrange("p (c i t) -> p c t i", t=4, i=2),
+                th[h, a][:, :, j0 : j0 + width].rearrange("p t (c i) -> p c t i", i=2),
+                sm_sb[:, a, :].unsqueeze(1).unsqueeze(3).to_broadcast([P, width // 2, 4, 2]),
                 ALU.mult,
             )
 
-        def quantise(h, a):
-            hq[h, a] = new([P, W], U32, f"hq{h}{a}")
-            hs[h, a] = new([P, W], U8, f"hs{h}{a}")
-            nc.vector.quantize_mx(out=hq[h, a][:].bitcast(FP8X4), scales=hs[h, a][:], in_=hb[h, a][:])
+        def quantise(h, a, j0=0, width=W):
+            if (h, a) not in hq:
+                hq[h, a] = new([P, W], U32, f"hq{h}{a}")
+                hs[h, a] = new([P, W], U8, f"hs{h}{a}")
+            nc.vector.quantize_mx(
+                out=hq[h, a][:, j0 : j0 + width].bitcast(FP8X4),
+                scales=hs[h, a][:, j0 : j0 + width],
+                in_=hb[h, a][:, 4 * j0 : 4 * (j0 + width)],
+            )
 
-        def score(h):
-            accs = [bank(c if h == 0 else (4 + c if c < 3 else 0)) for c in range(4)]
+        def score_pass(acc, h, a, c, cols, start, stop):
+            nc.tensor.matmul_mx(
+                out=acc,
+                lhsT=en_w[:].bitcast(U8)[:, a, 2 * c * P : 2 * (c + 1) * P].bitcast(FP4X4),
+                lhsT_scale=en_s[:].bitcast(U8)[:, a, c * P : (c + 1) * P],
+                rhs=hq[h, a][:, cols].bitcast(FP8X4),
+                rhs_scale=hs[h, a][:, cols],
+                start=start,
+                stop=stop,
+            )
+
+        def score_first():
+            accs = [bank(c) for c in range(4)]
             for a in range(2):
                 for c in range(4):
-                    nc.tensor.matmul_mx(
-                        out=accs[c][:],
-                        lhsT=en_w[:].bitcast(U8)[:, a, 2 * c * P : 2 * (c + 1) * P].bitcast(FP4X4),
-                        lhsT_scale=en_s[:].bitcast(U8)[:, a, c * P : (c + 1) * P],
-                        rhs=hq[h, a][:].bitcast(FP8X4),
-                        rhs_scale=hs[h, a][:],
-                        start=(a == 0),
-                        stop=(a == 1),
-                    )
+                    score_pass(accs[c][:], 0, a, c, slice(0, W), a == 0, a == 1)
             for c in range(4):
-                y = new([P, W], F32, f"y{h}{c}")
-                if h == 1 and c % 2 == 1:
-                    nc.vector.tensor_scalar_add(y[:], accs[c][:], b_sb[:, c : c + 1])
-                else:
-                    nc.scalar.activation(out=y[:], in_=accs[c][:], func=ACT.Identity, bias=b_sb[:, c : c + 1])
-                nc.sync.dma_start(out[c * P : (c + 1) * P, h * W : (h + 1) * W], y[:])
+                y = new([P, W], F32, f"y0{c}")
+                nc.scalar.activation(out=y[:], in_=accs[c][:], func=ACT.Identity, bias=b_sb[:, c : c + 1])
+                nc.sync.dma_start(out[c * P : (c + 1) * P, 0:W], y[:])
+
+        piece = {}
+
+        def score_piece(k, a):
+            if a == 0:
+                piece[k] = bank(4 + k)[:].rearrange("p (c j) -> p c j", c=4)
+            for c in range(4):
+                score_pass(piece[k][:, c, :], 1, a, c, slice(k * P, (k + 1) * P), (a, c) == (0, 0), (a, c) == (1, 3))
+
+        def store_piece(k):
+            y = new([P, 4, P], F32, f"y1{k}")
+            if k == 3:
+                nc.vector.tensor_tensor(y[:], piece[k], b_sb[:].unsqueeze(2).to_broadcast([P, 4, P]), ALU.add)
+            else:
+                for c in range(4):
+                    nc.scalar.activation(out=y[:, c, :], in_=piece[k][:, c, :], func=ACT.Identity, bias=b_sb[:, c : c + 1])
+            nc.sync.dma_start(out[:, W + k * P : W + (k + 1) * P].rearrange("(c p) j -> p c j", p=P), y[:])
 
         gather1_scales()
         gather1_words(0)
-        part(0)
+        part_both(0)
         permute_wa(0)
-        warm_acc = bank(4)
-        for i in range(3):
-            nc.tensor.matmul_mx(
-                out=warm_acc[:],
-                lhsT=wa_p[0][:, 0, 0:P].bitcast(FP8X4),
-                lhsT_scale=wa_s[:, 0, :].bitcast(U8)[:, 0:P],
-                rhs=v_w[0][:, 0, :].bitcast(FP4X4),
-                rhs_scale=g_s[:, 0:W],
-                start=True,
-                stop=True,
-            )
         for a in range(2):
             for g in range(2):
                 permute_scales(g, a, wa_s[:, g, :])
         for a in range(2):
             permute_scales(2, a, wb_s[:])
+        passes(0, 0, [(t, g) for g in range(2) for t in range(4)])
         gather1_words(1)
-        part(1)
-        for g in range(2):
-            for h in range(2):
-                passes(h, 0, [(t, g) for t in range(4 - h)])
+        part(1, 0)
+        passes(1, 0, [(t, 0) for t in range(4)])
         gather2_scales(0)
         gather2_words(0)
         permute_wb()
@@ -267,6 +264,7 @@ def tile_list_kg_tanh_bias_kernel(
         passes(0, 1, [(t, g) for t in range(4) for g in range(3)])
         gather2_scales(1)
         gather2_words(1)
+        part(1, 1)
         en_s = new([P, 2, N // 4], I32, "en_s")
         en_w = new([P, 2, N // 2], I32, "en_w")
         nc.sync.dma_start(en_w[:], en_words.rearrange("a p n -> p a n").bitcast(I32))
@@ -278,15 +276,21 @@ def tile_list_kg_tanh_bias_kernel(
         b_sb = new([P, 4], F32, "b_sb")
         with nc.allow_non_contiguous_dma(reason="one bias value to a partition"):
             nc.sync.dma_start(b_sb[:], b.rearrange("(c p) -> p c", p=P))
-        passes(1, 0, [(t, 2) for t in range(3)] + [(3, g) for g in range(3)])
+        passes(1, 0, [(t, g) for t in range(4) for g in range(1, 3)])
         passes(1, 1, [(t, g) for t in range(4) for g in range(3)])
         smooth(0, 0)
         smooth(0, 1)
         quantise(0, 0)
-        quantise(0, 1)
         smooth(1, 0)
-        score(0)
+        quantise(0, 1)
         quantise(1, 0)
-        smooth(1, 1)
-        quantise(1, 1)
-        score(1)
+        score_first()
+        smooth(1, 1, 0, P)
+        for k in range(4):
+            score_piece(k, 0)
+        for k in range(4):
+            if k < 3:
+                smooth(1, 1, (k + 1) * P, P)
+            quantise(1, 1, k * P, P)
+            score_piece(k, 1)
+            store_piece(k)

@@ -19,10 +19,9 @@ ALU = mybir.AluOpType
 P = 128
 W = 512
 PLACE = {
-    "tab_w": 16384, "g_s20": 16384,
+    "g_w0": 8192, "g_w1": 8192,
+    "tab_w": 16384, "g_w20": 16384, "g_s20": 18432,
     "wb_w": 4096, "g_s21": 4096, "g_w21": 5120,
-    "wa_w1": 10240, "v_w11": 10240,
-    "v_s0": 8192, "warm_out": 9152, "v_s1": 9216,
 }
 
 
@@ -47,35 +46,36 @@ def tile_list_kg_tanh_bias_kernel(
         list1 = keep.tile([P, J // 16], U16, name="list1")
         list2 = keep.tile([P, J // 16], U16, name="list2")
         sm_sb = new([P, 2, 4], F32, "sm_sb")
-        warm_out = new([P, 32], F32, "warm_out")
         tab_s = new([P, T // 4], I32, "tab_s")
         tab2_s = new([P, T // 4], I32, "tab2_s")
         wa_s = new([P, 2, R // 4], I32, "wa_s")
         wb_s = new([P, R // 4], I32, "wb_s")
         tab_w = new([P, T], I32, "tab_w")
         tab2_w = new([P, T], I32, "tab2_w")
-        wa_w = {0: new([P, 2, W], I32, "wa_w0")}
+        wa_w = {(0, g): new([P, W], I32, f"wa_w0{g}")[:] for g in range(2)}
         wb_w = new([P, R // 2], I32, "wb_w")
 
+        nc.gpsimd.memset(tab_s[:], 0)
         nc.vector.memset(wa_s[:], 0)
-        for q in range(4):
-            (nc.vector if q % 2 == 0 else nc.gpsimd).memset(tab_s[32 * q : 32 * q + 24, :], 0)
-        nc.gpsimd.memset(tab2_s[:], 0)
-        nc.gpsimd.memset(wb_s[:], 0)
+        nc.vector.memset(tab2_s[:], 0)
+        nc.vector.memset(wb_s[:], 0)
 
         wa_i = wa_words.rearrange("a p r i -> p a (r i)").bitcast(I32)
         nc.sync.dma_start(list1[:], offs)
+        nc.sync.dma_start(wa_w[0, 0], wa_i[:, 0, 0:W])
         for q in range(4):
-            nc.sync.dma_start(tab_s[32 * q + 24 : 32 * q + 32, :], tab_scales[:, 4 * q : 4 * q + 4, :].bitcast(I32))
+            nc.sync.dma_start(tab_s[32 * q : 32 * q + 8, :], tab_scales[:, 4 * q : 4 * q + 4, :].bitcast(I32))
         nc.sync.dma_start(tab_w[:], tab_words[0].rearrange("p t i -> p (t i)").bitcast(I32))
-        nc.sync.dma_start(sm_sb[:], sm.rearrange("(a p t) -> p a t", a=2, t=4))
-        nc.sync.dma_start(wa_w[0][:], wa_i[:, :, 0:W])
-        nc.scalar.activation(out=warm_out[:, 0:1], in_=sm_sb[:, 0, 0:1], func=ACT.Tanh)
         for q in range(4):
             nc.sync.dma_start(
                 wa_s[32 * q : 32 * q + 4, :, :],
                 wa_scales[:, 4 * q : 4 * q + 4, :].rearrange("a r n -> r a n").bitcast(I32),
             )
+        nc.sync.dma_start(wa_w[0, 1], wa_i[:, 1, 0:W])
+        wa_w1 = new([P, 2, W], I32, "wa_w1")
+        nc.sync.dma_start(wa_w1[:], wa_i[:, :, W : 2 * W])
+        for g in range(2):
+            wa_w[1, g] = wa_w1[:, g, :]
         nc.sync.dma_start(tab2_w[:], tab2_words[0].rearrange("p t i -> p (t i)").bitcast(I32))
         nc.sync.dma_start(list2[:], offs2)
         for q in range(4):
@@ -83,12 +83,12 @@ def tile_list_kg_tanh_bias_kernel(
         nc.sync.dma_start(wb_w[:], wb_words[0].bitcast(I32))
         for q in range(4):
             nc.sync.dma_start(wb_s[32 * q : 32 * q + 4, :], wb_scales[0, 4 * q : 4 * q + 4, :].bitcast(I32))
-        wa_w[1] = new([P, 2, W], I32, "wa_w1")
-        nc.sync.dma_start(wa_w[1][:], wa_i[:, :, W : 2 * W])
+        nc.sync.dma_start(sm_sb[:], sm.rearrange("(a p t) -> p a t", a=2, t=4))
 
-        v_s = [new([P, J // 4], I32, f"v_s{g}") for g in range(2)]
+        moved_s = new([P, J // 4], I32, "moved_s")
 
         g_s = new([P, J], U8, "g_s")
+        v_s = [g_s[:], moved_s[:].bitcast(U8)]
         g_s2 = {}
         g_w = {}
         g_w2 = {}
@@ -106,8 +106,7 @@ def tile_list_kg_tanh_bias_kernel(
 
         def gather1_scales():
             nc.vector.tensor_copy(g_s[:], tab_s[:].bitcast(U8).indirect(list1[:]))
-            for g in range(2):
-                nc.scalar.dma_start(v_s[g][0:100, :], g_s[24 + 4 * g : 124 + 4 * g, :].bitcast(I32))
+            nc.scalar.dma_start(moved_s[0:100, :], g_s[4:104, :].bitcast(I32))
 
         def gather1_words(h):
             cols = slice(h * W // 16, (h + 1) * W // 16)
@@ -142,11 +141,11 @@ def tile_list_kg_tanh_bias_kernel(
                 wb_w[:].bitcast(U16).rearrange("p (a c i t) -> p a c t i", a=2, t=4, i=8),
             )
 
-        def permute_wa(a):
-            wa_p[a] = new([P, 2, W], I32, f"wa_p{a}")
+        def permute_wa(a, g):
+            wa_p[a, g] = new([P, W], I32, f"wa_p{a}{g}")
             nc.gpsimd.tensor_copy(
-                wa_p[a][:].rearrange("p g (t c i) -> p g c t i", t=4, i=4),
-                wa_w[a][:].rearrange("p g (c i t) -> p g c t i", t=4, i=4),
+                wa_p[a, g][:].rearrange("p (t c i) -> p c t i", t=4, i=4),
+                wa_w[a, g].rearrange("p (c i t) -> p c t i", t=4, i=4),
             )
 
         th = {}
@@ -158,11 +157,11 @@ def tile_list_kg_tanh_bias_kernel(
         def one_pass(h, a, t, g):
             m = slice(t * P, (t + 1) * P)
             if g == 0:
-                z[h, a, t] = bank(4 + t if (h, a) == (1, 0) else t)
+                z[h, a, t] = bank(4 * a + t)
             if g < 2:
-                lhs = wa_p[a][:, g, m].bitcast(FP8X4)
+                lhs = wa_p[a, g][:, m].bitcast(FP8X4)
                 rhs = v_w[h, g].bitcast(FP4X4)
-                rhs_scale = v_s[g][:].bitcast(U8)[:, h * W : (h + 1) * W]
+                rhs_scale = v_s[g][:, h * W : (h + 1) * W]
             else:
                 lhs = wb_p[0][:, a, 2 * t * P : 2 * (t + 1) * P].bitcast(FP4X4)
                 rhs = g_w2[h][:].bitcast(FP8X4)
@@ -216,15 +215,17 @@ def tile_list_kg_tanh_bias_kernel(
                 stop=stop,
             )
 
-        def score_first():
-            accs = [bank(c) for c in range(4)]
-            for a in range(2):
-                for c in range(4):
-                    score_pass(accs[c][:], 0, a, c, slice(0, W), a == 0, a == 1)
+        accs = {}
+
+        def score_first(a):
             for c in range(4):
-                y = new([P, W], F32, f"y0{c}")
-                nc.scalar.activation(out=y[:], in_=accs[c][:], func=ACT.Identity, bias=b_sb[:, c : c + 1])
-                nc.sync.dma_start(out[c * P : (c + 1) * P, 0:W], y[:])
+                if a == 0:
+                    accs[c] = bank(c)
+                score_pass(accs[c][:], 0, a, c, slice(0, W), a == 0, a == 1)
+                if a == 1:
+                    y = new([P, W], F32, f"y0{c}")
+                    nc.scalar.activation(out=y[:], in_=accs[c][:], func=ACT.Identity, bias=b_sb[:, c : c + 1])
+                    nc.sync.dma_start(out[c * P : (c + 1) * P, 0:W], y[:])
 
         piece = {}
 
@@ -236,7 +237,7 @@ def tile_list_kg_tanh_bias_kernel(
 
         def store_piece(k):
             y = new([P, 4, P], F32, f"y1{k}")
-            if k == 3:
+            if k >= 2:
                 nc.vector.tensor_tensor(y[:], piece[k], b_sb[:].unsqueeze(2).to_broadcast([P, 4, P]), ALU.add)
             else:
                 for c in range(4):
@@ -245,26 +246,28 @@ def tile_list_kg_tanh_bias_kernel(
 
         gather1_scales()
         gather1_words(0)
-        part_both(0)
-        permute_wa(0)
+        part(0, 0)
+        part(0, 1)
+        permute_wa(0, 0)
+        permute_scales(0, 0, wa_s[:, 0, :])
+        permute_wa(0, 1)
+        permute_scales(1, 0, wa_s[:, 1, :])
+        for g in range(2):
+            permute_scales(g, 1, wa_s[:, g, :])
+            permute_wa(1, g)
         for a in range(2):
-            for g in range(2):
-                permute_scales(g, a, wa_s[:, g, :])
+            passes(0, a, [(t, g) for g in range(2) for t in range(4)])
+        gather1_words(1)
+        part_both(1)
+        gather2_words(0)
+        gather2_scales(0)
+        permute_wb()
         for a in range(2):
             permute_scales(2, a, wb_s[:])
-        passes(0, 0, [(t, g) for g in range(2) for t in range(4)])
-        gather1_words(1)
-        part(1, 0)
-        passes(1, 0, [(t, 0) for t in range(4)])
-        gather2_scales(0)
-        gather2_words(0)
-        permute_wb()
-        passes(0, 0, [(t, 2) for t in range(4)])
-        permute_wa(1)
-        passes(0, 1, [(t, g) for t in range(4) for g in range(3)])
-        gather2_scales(1)
+            passes(0, a, [(t, 2) for t in range(4)])
         gather2_words(1)
-        part(1, 1)
+        gather2_scales(1)
+        passes(1, 0, [(t, g) for t in range(4) for g in range(3)])
         en_s = new([P, 2, N // 4], I32, "en_s")
         en_w = new([P, 2, N // 2], I32, "en_w")
         nc.sync.dma_start(en_w[:], en_words.rearrange("a p n -> p a n").bitcast(I32))
@@ -276,21 +279,20 @@ def tile_list_kg_tanh_bias_kernel(
         b_sb = new([P, 4], F32, "b_sb")
         with nc.allow_non_contiguous_dma(reason="one bias value to a partition"):
             nc.sync.dma_start(b_sb[:], b.rearrange("(c p) -> p c", p=P))
-        passes(1, 0, [(t, g) for t in range(4) for g in range(1, 3)])
         passes(1, 1, [(t, g) for t in range(4) for g in range(3)])
-        smooth(0, 0)
-        smooth(0, 1)
-        quantise(0, 0)
-        smooth(1, 0)
-        quantise(0, 1)
-        quantise(1, 0)
-        score_first()
-        smooth(1, 1, 0, P)
+        for h, a in ((0, 0), (0, 1), (1, 0)):
+            for step in (smooth, quantise):
+                for j0 in (0, W // 2):
+                    step(h, a, j0, W // 2)
+        for a in range(2):
+            score_first(a)
         for k in range(4):
             score_piece(k, 0)
+        smooth(1, 1, 0, P)
         for k in range(4):
             if k < 3:
                 smooth(1, 1, (k + 1) * P, P)
             quantise(1, 1, k * P, P)
             score_piece(k, 1)
+        for k in range(4):
             store_piece(k)

@@ -63,14 +63,11 @@ def tile_list_kg_tanh_bias_kernel(
         wa_i = wa_words.rearrange("a p r i -> p a (r i)").bitcast(I32)
         nc.sync.dma_start(list1[:], offs)
         nc.sync.dma_start(wa_w[0, 0], wa_i[:, 0, 0:W])
-        for q in range(4):
-            nc.sync.dma_start(tab_s[32 * q : 32 * q + 8, :], tab_scales[:, 4 * q : 4 * q + 4, :].bitcast(I32))
+        for r in range(4):
+            nc.sync.dma_start(tab_s[r:P:16, :], tab_scales.rearrange("a (q r) t -> r q a t", r=4)[r].bitcast(I32))
         nc.sync.dma_start(tab_w[:], tab_words[0].rearrange("p t i -> p (t i)").bitcast(I32))
-        for q in range(4):
-            nc.sync.dma_start(
-                wa_s[32 * q : 32 * q + 4, :, :],
-                wa_scales[:, 4 * q : 4 * q + 4, :].rearrange("a r n -> r a n").bitcast(I32),
-            )
+        for r in range(4):
+            nc.sync.dma_start(wa_s[r:P:32, :, :], wa_scales.rearrange("a (q r) n -> r q a n", r=4)[r].bitcast(I32))
         nc.sync.dma_start(wa_w[0, 1], wa_i[:, 1, 0:W])
         wa_w1 = new([P, 2, W], I32, "wa_w1")
         nc.sync.dma_start(wa_w1[:], wa_i[:, :, W : 2 * W])
@@ -78,11 +75,11 @@ def tile_list_kg_tanh_bias_kernel(
             wa_w[1, g] = wa_w1[:, g, :]
         nc.sync.dma_start(tab2_w[:], tab2_words[0].rearrange("p t i -> p (t i)").bitcast(I32))
         nc.sync.dma_start(list2[:], offs2)
-        for q in range(4):
-            nc.sync.dma_start(tab2_s[32 * q : 32 * q + 4, :], tab2_scales[0, 4 * q : 4 * q + 4, :].bitcast(I32))
+        for r in range(4):
+            nc.sync.dma_start(tab2_s[r:P:32, :], tab2_scales[0, r:16:4, :].bitcast(I32))
         nc.sync.dma_start(wb_w[:], wb_words[0].bitcast(I32))
-        for q in range(4):
-            nc.sync.dma_start(wb_s[32 * q : 32 * q + 4, :], wb_scales[0, 4 * q : 4 * q + 4, :].bitcast(I32))
+        for r in range(4):
+            nc.sync.dma_start(wb_s[r:P:32, :], wb_scales[0, r:16:4, :].bitcast(I32))
         nc.sync.dma_start(sm_sb[:], sm.rearrange("(a p t) -> p a t", a=2, t=4))
 
         moved_s = new([P, J // 4], I32, "moved_s")
@@ -106,7 +103,7 @@ def tile_list_kg_tanh_bias_kernel(
 
         def gather1_scales():
             nc.vector.tensor_copy(g_s[:], tab_s[:].bitcast(U8).indirect(list1[:]))
-            nc.scalar.dma_start(moved_s[0:100, :], g_s[4:104, :].bitcast(I32))
+            nc.scalar.dma_start(moved_s[0:100, :], g_s[16:116, :].bitcast(I32))
 
         def gather1_words(h):
             cols = slice(h * W // 16, (h + 1) * W // 16)
@@ -271,11 +268,8 @@ def tile_list_kg_tanh_bias_kernel(
         en_s = new([P, 2, N // 4], I32, "en_s")
         en_w = new([P, 2, N // 2], I32, "en_w")
         nc.sync.dma_start(en_w[:], en_words.rearrange("a p n -> p a n").bitcast(I32))
-        for q in range(4):
-            nc.sync.dma_start(
-                en_s[32 * q : 32 * q + 4, :, :],
-                en_scales[:, 4 * q : 4 * q + 4, :].rearrange("a r n -> r a n").bitcast(I32),
-            )
+        for r in range(4):
+            nc.sync.dma_start(en_s[r:P:32, :, :], en_scales.rearrange("a (q r) n -> r q a n", r=4)[r].bitcast(I32))
         b_sb = new([P, 4], F32, "b_sb")
         with nc.allow_non_contiguous_dma(reason="one bias value to a partition"):
             nc.sync.dma_start(b_sb[:], b.rearrange("(c p) -> p c", p=P))

@@ -140,7 +140,7 @@ def tile_list_kg_tanh_bias_kernel(
 
         def permute_wa(a, g):
             wa_p[a, g] = new([P, W], I32, f"wa_p{a}{g}")
-            nc.gpsimd.tensor_copy(
+            nc.vector.tensor_copy(
                 wa_p[a, g][:].rearrange("p (t c i) -> p c t i", t=4, i=4),
                 wa_w[a, g].rearrange("p (c i t) -> p c t i", t=4, i=4),
             )

@@ -19,6 +19,7 @@ ALU = mybir.AluOpType
 P = 128
 W = 512
 PLACE = {
+    "hb01_256": 24576, "hq10": 24576,
     "g_w0": 8192, "g_w1": 8192,
     "tab_w": 16384, "g_w20": 16384, "g_s20": 18432,
     "wb_w": 4096, "g_s21": 4096, "g_w21": 5120,
@@ -69,10 +70,6 @@ def tile_list_kg_tanh_bias_kernel(
         for r in range(4):
             nc.sync.dma_start(wa_s[r:P:32, :, :], wa_scales.rearrange("a (q r) n -> r q a n", r=4)[r].bitcast(I32))
         nc.sync.dma_start(wa_w[0, 1], wa_i[:, 1, 0:W])
-        wa_w1 = new([P, 2, W], I32, "wa_w1")
-        nc.sync.dma_start(wa_w1[:], wa_i[:, :, W : 2 * W])
-        for g in range(2):
-            wa_w[1, g] = wa_w1[:, g, :]
         nc.sync.dma_start(tab2_w[:], tab2_words[0].rearrange("p t i -> p (t i)").bitcast(I32))
         nc.sync.dma_start(list2[:], offs2)
         for r in range(4):
@@ -80,6 +77,10 @@ def tile_list_kg_tanh_bias_kernel(
         nc.sync.dma_start(wb_w[:], wb_words[0].bitcast(I32))
         for r in range(4):
             nc.sync.dma_start(wb_s[r:P:32, :], wb_scales[0, r:16:4, :].bitcast(I32))
+        wa_w1 = new([P, 2, W], I32, "wa_w1")
+        nc.sync.dma_start(wa_w1[:], wa_i[:, :, W : 2 * W])
+        for g in range(2):
+            wa_w[1, g] = wa_w1[:, g, :]
         nc.sync.dma_start(sm_sb[:], sm.rearrange("(a p t) -> p a t", a=2, t=4))
 
         moved_s = new([P, J // 4], I32, "moved_s")
@@ -154,7 +155,7 @@ def tile_list_kg_tanh_bias_kernel(
         def one_pass(h, a, t, g):
             m = slice(t * P, (t + 1) * P)
             if g == 0:
-                z[h, a, t] = bank(4 * a + t)
+                z[h, a, t] = bank(4 * h + t)
             if g < 2:
                 lhs = wa_p[a, g][:, m].bitcast(FP8X4)
                 rhs = v_w[h, g].bitcast(FP4X4)
@@ -182,10 +183,9 @@ def tile_list_kg_tanh_bias_kernel(
                 one_pass(h, a, t, g)
 
         def smooth(h, a, j0=0, width=W):
-            if (h, a) not in hb:
-                hb[h, a] = new([P, 4 * W], BF16, f"hb{h}{a}")
+            hb[h, a, j0] = new([P, 4 * width], BF16, f"hb{h}{a}_{j0}")
             nc.vector.tensor_tensor(
-                hb[h, a][:, 4 * j0 : 4 * (j0 + width)].rearrange("p (c i t) -> p c t i", t=4, i=2),
+                hb[h, a, j0][:].rearrange("p (c i t) -> p c t i", t=4, i=2),
                 th[h, a][:, :, j0 : j0 + width].rearrange("p t (c i) -> p c t i", i=2),
                 sm_sb[:, a, :].unsqueeze(1).unsqueeze(3).to_broadcast([P, width // 2, 4, 2]),
                 ALU.mult,
@@ -198,7 +198,7 @@ def tile_list_kg_tanh_bias_kernel(
             nc.vector.quantize_mx(
                 out=hq[h, a][:, j0 : j0 + width].bitcast(FP8X4),
                 scales=hs[h, a][:, j0 : j0 + width],
-                in_=hb[h, a][:, 4 * j0 : 4 * (j0 + width)],
+                in_=hb[h, a, j0][:],
             )
 
         def score_pass(acc, h, a, c, cols, start, stop):
@@ -234,7 +234,7 @@ def tile_list_kg_tanh_bias_kernel(
 
         def store_piece(k):
             y = new([P, 4, P], F32, f"y1{k}")
-            if k >= 2:
+            if k == 3:
                 nc.vector.tensor_tensor(y[:], piece[k], b_sb[:].unsqueeze(2).to_broadcast([P, 4, P]), ALU.add)
             else:
                 for c in range(4):
@@ -249,22 +249,25 @@ def tile_list_kg_tanh_bias_kernel(
         permute_scales(0, 0, wa_s[:, 0, :])
         permute_wa(0, 1)
         permute_scales(1, 0, wa_s[:, 1, :])
-        for g in range(2):
-            permute_scales(g, 1, wa_s[:, g, :])
-            permute_wa(1, g)
-        for a in range(2):
-            passes(0, a, [(t, g) for g in range(2) for t in range(4)])
         gather1_words(1)
         part_both(1)
+        for g in range(2):
+            for h in range(2):
+                passes(h, 0, [(t, g) for t in range(4)])
         gather2_words(0)
         gather2_scales(0)
         permute_wb()
-        for a in range(2):
-            permute_scales(2, a, wb_s[:])
-            passes(0, a, [(t, 2) for t in range(4)])
+        permute_scales(2, 0, wb_s[:])
+        passes(0, 0, [(t, 2) for t in range(4)])
         gather2_words(1)
         gather2_scales(1)
-        passes(1, 0, [(t, g) for t in range(4) for g in range(3)])
+        passes(1, 0, [(t, 2) for t in range(4)])
+        for g in range(2):
+            permute_scales(g, 1, wa_s[:, g, :])
+        for g in range(2):
+            permute_wa(1, g)
+        permute_scales(2, 1, wb_s[:])
+        passes(0, 1, [(t, g) for t in range(4) for g in range(3)])
         en_s = new([P, 2, N // 4], I32, "en_s")
         en_w = new([P, 2, N // 2], I32, "en_w")
         nc.sync.dma_start(en_w[:], en_words.rearrange("a p n -> p a n").bitcast(I32))
@@ -274,10 +277,17 @@ def tile_list_kg_tanh_bias_kernel(
         with nc.allow_non_contiguous_dma(reason="one bias value to a partition"):
             nc.sync.dma_start(b_sb[:], b.rearrange("(c p) -> p c", p=P))
         passes(1, 1, [(t, g) for t in range(4) for g in range(3)])
-        for h, a in ((0, 0), (0, 1), (1, 0)):
-            for step in (smooth, quantise):
-                for j0 in (0, W // 2):
-                    step(h, a, j0, W // 2)
+        half = W // 2
+        for step in (smooth, quantise):
+            for j0 in (0, half):
+                step(0, 0, j0, half)
+        for j0 in (0, half):
+            smooth(1, 0, j0, half)
+        for step in (smooth, quantise):
+            for j0 in (0, half):
+                step(0, 1, j0, half)
+        for j0 in (0, half):
+            quantise(1, 0, j0, half)
         for a in range(2):
             score_first(a)
         for k in range(4):

@@ -141,7 +141,7 @@ def tile_list_kg_tanh_bias_kernel(
 
         def permute_wa(a, g):
             wa_p[a, g] = new([P, W], I32, f"wa_p{a}{g}")
-            nc.vector.tensor_copy(
+            (nc.gpsimd if (a, g) == (0, 1) else nc.vector).tensor_copy(
                 wa_p[a, g][:].rearrange("p (t c i) -> p c t i", t=4, i=4),
                 wa_w[a, g].rearrange("p (c i t) -> p c t i", t=4, i=4),
             )
@@ -191,6 +191,23 @@ def tile_list_kg_tanh_bias_kernel(
                 ALU.mult,
             )
 
+        planes = {}
+
+        def scale_planes(h, a, j0, width):
+            planes[h, a] = (j0, new([P, 4, width], BF16, f"planes{h}{a}"))
+            for t in range(4):
+                nc.scalar.activation(
+                    out=planes[h, a][1][:, t, :], in_=th[h, a][:, t, j0 : j0 + width], func=ACT.Copy, scale=sm_sb[:, a, t : t + 1]
+                )
+
+        def weave(h, a, j0, width):
+            first, src = planes[h, a]
+            hb[h, a, j0] = new([P, 4 * width], BF16, f"hb{h}{a}_{j0}")
+            nc.vector.tensor_copy(
+                hb[h, a, j0][:].rearrange("p (c i t) -> p c t i", t=4, i=4),
+                src[:, :, j0 - first : j0 - first + width].rearrange("p t (c i) -> p c t i", i=4),
+            )
+
         def quantise(h, a, j0=0, width=W):
             if (h, a) not in hq:
                 hq[h, a] = new([P, W], U32, f"hq{h}{a}")
@@ -234,7 +251,7 @@ def tile_list_kg_tanh_bias_kernel(
 
         def store_piece(k):
             y = new([P, 4, P], F32, f"y1{k}")
-            if k == 3:
+            if k >= 2:
                 nc.vector.tensor_tensor(y[:], piece[k], b_sb[:].unsqueeze(2).to_broadcast([P, 4, P]), ALU.add)
             else:
                 for c in range(4):
@@ -278,6 +295,7 @@ def tile_list_kg_tanh_bias_kernel(
             nc.sync.dma_start(b_sb[:], b.rearrange("(c p) -> p c", p=P))
         passes(1, 1, [(t, g) for t in range(4) for g in range(3)])
         half = W // 2
+        scale_planes(1, 1, half, half)
         for step in (smooth, quantise):
             for j0 in (0, half):
                 step(0, 0, j0, half)
@@ -295,7 +313,7 @@ def tile_list_kg_tanh_bias_kernel(
         smooth(1, 1, 0, P)
         for k in range(4):
             if k < 3:
-                smooth(1, 1, (k + 1) * P, P)
+                (smooth if k == 0 else weave)(1, 1, (k + 1) * P, P)
             quantise(1, 1, k * P, P)
             score_piece(k, 1)
         for k in range(4):

@@ -22,7 +22,6 @@ PLACE = {
     "hb01_256": 24576, "hq10": 24576,
     "g_w0": 8192, "g_w1": 8192,
     "tab_w": 16384, "g_w20": 16384, "g_s20": 18432,
-    "wb_w": 4096, "g_s21": 4096, "g_w21": 5120,
 }
 
 
@@ -62,26 +61,24 @@ def tile_list_kg_tanh_bias_kernel(
         nc.vector.memset(wb_s[:], 0)
 
         wa_i = wa_words.rearrange("a p r i -> p a (r i)").bitcast(I32)
+
+        def load_rows(dst, src, rows, step):
+            for r in rows:
+                nc.sync.dma_start(dst[r:P:step], src[r].bitcast(I32))
+
+        tab_rows = tab_scales.rearrange("a (q r) t -> r q a t", r=4)
+        tab2_rows = tab2_scales[0].rearrange("(q r) t -> r q t", r=4)
+        wa_rows = wa_scales.rearrange("a (q r) n -> r q a n", r=4)
+        wb_rows = wb_scales[0].rearrange("(q r) n -> r q n", r=4)
         nc.sync.dma_start(list1[:], offs)
         nc.sync.dma_start(wa_w[0, 0], wa_i[:, 0, 0:W])
-        for r in range(4):
-            nc.sync.dma_start(tab_s[r:P:16, :], tab_scales.rearrange("a (q r) t -> r q a t", r=4)[r].bitcast(I32))
+        load_rows(tab_s, tab_rows, range(4), 16)
+        load_rows(wa_s, wa_rows, [0], 32)
         nc.sync.dma_start(tab_w[:], tab_words[0].rearrange("p t i -> p (t i)").bitcast(I32))
-        for r in range(4):
-            nc.sync.dma_start(wa_s[r:P:32, :, :], wa_scales.rearrange("a (q r) n -> r q a n", r=4)[r].bitcast(I32))
-        nc.sync.dma_start(wa_w[0, 1], wa_i[:, 1, 0:W])
-        nc.sync.dma_start(tab2_w[:], tab2_words[0].rearrange("p t i -> p (t i)").bitcast(I32))
+        load_rows(wa_s, wa_rows, [1, 2, 3], 32)
         nc.sync.dma_start(list2[:], offs2)
-        for r in range(4):
-            nc.sync.dma_start(tab2_s[r:P:32, :], tab2_scales[0, r:16:4, :].bitcast(I32))
-        nc.sync.dma_start(wb_w[:], wb_words[0].bitcast(I32))
-        for r in range(4):
-            nc.sync.dma_start(wb_s[r:P:32, :], wb_scales[0, r:16:4, :].bitcast(I32))
-        wa_w1 = new([P, 2, W], I32, "wa_w1")
-        nc.sync.dma_start(wa_w1[:], wa_i[:, :, W : 2 * W])
-        for g in range(2):
-            wa_w[1, g] = wa_w1[:, g, :]
-        nc.sync.dma_start(sm_sb[:], sm.rearrange("(a p t) -> p a t", a=2, t=4))
+        load_rows(tab2_s, tab2_rows, [0, 1], 32)
+        nc.sync.dma_start(tab2_w[:], tab2_words[0].rearrange("p t i -> p (t i)").bitcast(I32))
 
         moved_s = new([P, J // 4], I32, "moved_s")
 
@@ -104,7 +101,7 @@ def tile_list_kg_tanh_bias_kernel(
 
         def gather1_scales():
             nc.vector.tensor_copy(g_s[:], tab_s[:].bitcast(U8).indirect(list1[:]))
-            nc.scalar.dma_start(moved_s[0:100, :], g_s[16:116, :].bitcast(I32))
+            nc.sync.dma_start(moved_s[0:100, :], g_s[16:116, :].bitcast(I32))
 
         def gather1_words(h):
             cols = slice(h * W // 16, (h + 1) * W // 16)
@@ -132,18 +129,18 @@ def tile_list_kg_tanh_bias_kernel(
                 src.bitcast(U8)[:, a * W : (a + 1) * W].rearrange("p (c i t) -> p c t i", t=4, i=16),
             )
 
-        def permute_wb():
-            wb_p[0] = new([P, 2, 2 * W], U8, "wb_p")
-            nc.vector.tensor_copy(
-                wb_p[0][:].bitcast(U16).rearrange("p a (t c i) -> p a c t i", t=4, i=8),
-                wb_w[:].bitcast(U16).rearrange("p (a c i t) -> p a c t i", a=2, t=4, i=8),
+        def permute_wb(a):
+            wb_p[a] = new([P, 2 * W], U8, f"wb_p{a}")
+            nc.scalar.copy(
+                wb_p[a][:].bitcast(U16).rearrange("p (t c i) -> p c t i", t=4, i=8),
+                wb_w[:].bitcast(U16)[:, a * W : (a + 1) * W].rearrange("p (c i t) -> p c t i", t=4, i=8),
             )
 
         def permute_wa(a, g):
-            wa_p[a, g] = new([P, W], I32, f"wa_p{a}{g}")
-            (nc.gpsimd if (a, g) == (0, 1) else nc.vector).tensor_copy(
+            wa_p[a, g] = new([P, W], U32, f"wa_p{a}{g}")
+            (nc.scalar.copy if a == 0 else nc.gpsimd.tensor_copy)(
                 wa_p[a, g][:].rearrange("p (t c i) -> p c t i", t=4, i=4),
-                wa_w[a, g].rearrange("p (c i t) -> p c t i", t=4, i=4),
+                wa_w[a, g].bitcast(U32).rearrange("p (c i t) -> p c t i", t=4, i=4),
             )
 
         th = {}
@@ -154,14 +151,15 @@ def tile_list_kg_tanh_bias_kernel(
 
         def one_pass(h, a, t, g):
             m = slice(t * P, (t + 1) * P)
-            if g == 0:
+            first, final = (0, 2) if a == 0 else (2, 1)
+            if g == first:
                 z[h, a, t] = bank(4 * h + t)
             if g < 2:
                 lhs = wa_p[a, g][:, m].bitcast(FP8X4)
                 rhs = v_w[h, g].bitcast(FP4X4)
                 rhs_scale = v_s[g][:, h * W : (h + 1) * W]
             else:
-                lhs = wb_p[0][:, a, 2 * t * P : 2 * (t + 1) * P].bitcast(FP4X4)
+                lhs = wb_p[a][:, 2 * t * P : 2 * (t + 1) * P].bitcast(FP4X4)
                 rhs = g_w2[h][:].bitcast(FP8X4)
                 rhs_scale = g_s2[h][:]
             nc.tensor.matmul_mx(
@@ -170,10 +168,10 @@ def tile_list_kg_tanh_bias_kernel(
                 lhsT_scale=ws_p[g, a][:, m],
                 rhs=rhs,
                 rhs_scale=rhs_scale,
-                start=(g == 0),
-                stop=(g == 2),
+                start=(g == first),
+                stop=(g == final),
             )
-            if g == 2:
+            if g == final:
                 nc.scalar.activation(out=th[h, a][:, t, :], in_=z[h, a, t][:], func=ACT.Tanh)
 
         def passes(h, a, order):
@@ -259,6 +257,15 @@ def tile_list_kg_tanh_bias_kernel(
             nc.sync.dma_start(out[:, W + k * P : W + (k + 1) * P].rearrange("(c p) j -> p c j", p=P), y[:])
 
         gather1_scales()
+        nc.sync.dma_start(wa_w[0, 1], wa_i[:, 1, 0:W])
+        load_rows(tab2_s, tab2_rows, [2, 3], 32)
+        nc.sync.dma_start(wb_w[:], wb_words[0].bitcast(I32))
+        load_rows(wb_s, wb_rows, range(4), 32)
+        wa_w1 = new([P, 2, W], I32, "wa_w1")
+        nc.sync.dma_start(wa_w1[:], wa_i[:, :, W : 2 * W])
+        for g in range(2):
+            wa_w[1, g] = wa_w1[:, g, :]
+        nc.sync.dma_start(sm_sb[:], sm.rearrange("(a p t) -> p a t", a=2, t=4))
         gather1_words(0)
         part(0, 0)
         part(0, 1)
@@ -273,7 +280,8 @@ def tile_list_kg_tanh_bias_kernel(
                 passes(h, 0, [(t, g) for t in range(4)])
         gather2_words(0)
         gather2_scales(0)
-        permute_wb()
+        for a in range(2):
+            permute_wb(a)
         permute_scales(2, 0, wb_s[:])
         passes(0, 0, [(t, 2) for t in range(4)])
         gather2_words(1)
@@ -281,10 +289,10 @@ def tile_list_kg_tanh_bias_kernel(
         passes(1, 0, [(t, 2) for t in range(4)])
         for g in range(2):
             permute_scales(g, 1, wa_s[:, g, :])
+        permute_scales(2, 1, wb_s[:])
         for g in range(2):
             permute_wa(1, g)
-        permute_scales(2, 1, wb_s[:])
-        passes(0, 1, [(t, g) for t in range(4) for g in range(3)])
+        passes(0, 1, [(t, 2) for t in range(4)] + [(t, g) for t in range(4) for g in range(2)])
         en_s = new([P, 2, N // 4], I32, "en_s")
         en_w = new([P, 2, N // 2], I32, "en_w")
         nc.sync.dma_start(en_w[:], en_words.rearrange("a p n -> p a n").bitcast(I32))
@@ -293,7 +301,7 @@ def tile_list_kg_tanh_bias_kernel(
         b_sb = new([P, 4], F32, "b_sb")
         with nc.allow_non_contiguous_dma(reason="one bias value to a partition"):
             nc.sync.dma_start(b_sb[:], b.rearrange("(c p) -> p c", p=P))
-        passes(1, 1, [(t, g) for t in range(4) for g in range(3)])
+        passes(1, 1, [(t, g) for t in range(4) for g in (2, 0, 1)])
         half = W // 2
         scale_planes(1, 1, half, half)
         for step in (smooth, quantise):

@@ -19,8 +19,8 @@ ALU = mybir.AluOpType
 P = 128
 W = 512
 PLACE = {
-    "hb01_256": 24576, "hq10": 24576,
-    "g_w0": 8192, "g_w1": 8192,
+    "g_w0_0": 512, "g_w0_256": 0, "g_w1_0": 1024,
+    "wa_w1": 4096, "g_w21": 4096, "g_s21": 6144,
     "tab_w": 16384, "g_w20": 16384, "g_s20": 18432,
 }
 
@@ -62,8 +62,8 @@ def tile_list_kg_tanh_bias_kernel(
 
         wa_i = wa_words.rearrange("a p r i -> p a (r i)").bitcast(I32)
 
-        def load_rows(dst, src, rows, step):
-            for r in rows:
+        def load_rows(dst, src, step):
+            for r in range(4):
                 nc.sync.dma_start(dst[r:P:step], src[r].bitcast(I32))
 
         tab_rows = tab_scales.rearrange("a (q r) t -> r q a t", r=4)
@@ -72,13 +72,20 @@ def tile_list_kg_tanh_bias_kernel(
         wb_rows = wb_scales[0].rearrange("(q r) n -> r q n", r=4)
         nc.sync.dma_start(list1[:], offs)
         nc.sync.dma_start(wa_w[0, 0], wa_i[:, 0, 0:W])
-        load_rows(tab_s, tab_rows, range(4), 16)
-        load_rows(wa_s, wa_rows, [0], 32)
+        load_rows(tab_s, tab_rows, 16)
         nc.sync.dma_start(tab_w[:], tab_words[0].rearrange("p t i -> p (t i)").bitcast(I32))
-        load_rows(wa_s, wa_rows, [1, 2, 3], 32)
-        nc.sync.dma_start(list2[:], offs2)
-        load_rows(tab2_s, tab2_rows, [0, 1], 32)
+        load_rows(wa_s, wa_rows, 32)
+        nc.sync.dma_start(wa_w[0, 1], wa_i[:, 1, 0:W])
         nc.sync.dma_start(tab2_w[:], tab2_words[0].rearrange("p t i -> p (t i)").bitcast(I32))
+        nc.sync.dma_start(list2[:], offs2)
+        load_rows(tab2_s, tab2_rows, 32)
+        nc.sync.dma_start(wb_w[:], wb_words[0].bitcast(I32))
+        load_rows(wb_s, wb_rows, 32)
+        wa_w1 = new([P, 2, W], I32, "wa_w1")
+        nc.sync.dma_start(wa_w1[:], wa_i[:, :, W : 2 * W])
+        for g in range(2):
+            wa_w[1, g] = wa_w1[:, g, :]
+        nc.sync.dma_start(sm_sb[:], sm.rearrange("(a p t) -> p a t", a=2, t=4))
 
         moved_s = new([P, J // 4], I32, "moved_s")
 
@@ -101,29 +108,31 @@ def tile_list_kg_tanh_bias_kernel(
 
         def gather1_scales():
             nc.vector.tensor_copy(g_s[:], tab_s[:].bitcast(U8).indirect(list1[:]))
-            nc.sync.dma_start(moved_s[0:100, :], g_s[16:116, :].bitcast(I32))
+            nc.scalar.dma_start(moved_s[0:100, :], g_s[16:116, :].bitcast(I32))
 
-        def gather1_words(h):
-            cols = slice(h * W // 16, (h + 1) * W // 16)
-            g_w[h] = new([P, W], U32, f"g_w{h}")
-            nc.vector.tensor_copy(g_w[h][:], tab_w[:].bitcast(U32).indirect(list1[:, cols]))
+        def gather1_words(h, j0=0, width=W):
+            first = h * W + j0
+            g_w[h, j0] = new([P, width], U32, f"g_w{h}_{j0}")
+            nc.vector.tensor_copy(g_w[h, j0][:], tab_w[:].bitcast(U32).indirect(list1[:, first // 16 : (first + width) // 16]))
 
-        def part_both(h):
-            both = new([P, 2, 2 * W], U8, f"v_w{h}")
-            nc.vector.tensor_copy(both[:].bitcast(U16), g_w[h][:].bitcast(U16).rearrange("p (j d) -> p d j", d=2))
-            v_w[h, 0] = both[:, 0, :]
-            v_w[h, 1] = both[:, 1, :]
+        parted = {}
 
-        def part(h, d):
-            one = new([P, 2 * W], U8, f"v_w{h}{d}")
-            nc.vector.tensor_copy(one[:].bitcast(U16), g_w[h][:].bitcast(U16).rearrange("p (j d) -> p d j", d=2)[:, d, :])
-            v_w[h, d] = one[:]
+        def part(h, j0=0, width=W):
+            if h not in parted:
+                parted[h] = new([P, 2, 2 * W], U8, f"v_w{h}")
+                for d in range(2):
+                    v_w[h, d] = parted[h][:, d, :]
+            nc.vector.tensor_copy(
+                parted[h][:].bitcast(U16)[:, :, j0 : j0 + width],
+                g_w[h, j0][:].bitcast(U16).rearrange("p (j d) -> p d j", d=2),
+            )
 
         wa_p = {}
         wb_p = {}
-        ws_p = {(g, a): new([P, W], U8, f"ws_p{g}{a}") for g in range(3) for a in range(2)}
+        ws_p = {}
 
         def permute_scales(g, a, src):
+            ws_p[g, a] = new([P, W], U8, f"ws_p{g}{a}")
             nc.gpsimd.tensor_copy(
                 ws_p[g, a][:].rearrange("p (t c i) -> p c t i", t=4, i=16),
                 src.bitcast(U8)[:, a * W : (a + 1) * W].rearrange("p (c i t) -> p c t i", t=4, i=16),
@@ -138,7 +147,7 @@ def tile_list_kg_tanh_bias_kernel(
 
         def permute_wa(a, g):
             wa_p[a, g] = new([P, W], U32, f"wa_p{a}{g}")
-            (nc.scalar.copy if a == 0 else nc.gpsimd.tensor_copy)(
+            (nc.scalar.copy if a == 0 else nc.vector.tensor_copy)(
                 wa_p[a, g][:].rearrange("p (t c i) -> p c t i", t=4, i=4),
                 wa_w[a, g].bitcast(U32).rearrange("p (c i t) -> p c t i", t=4, i=4),
             )
@@ -149,26 +158,27 @@ def tile_list_kg_tanh_bias_kernel(
         hs = {}
         z = {}
 
-        def one_pass(h, a, t, g):
+        def one_pass(h, a, t, g, j0=0, width=W):
             m = slice(t * P, (t + 1) * P)
+            js = slice(j0, j0 + width)
             first, final = (0, 2) if a == 0 else (2, 1)
-            if g == first:
+            if g == first and j0 == 0:
                 z[h, a, t] = bank(4 * h + t)
             if g < 2:
                 lhs = wa_p[a, g][:, m].bitcast(FP8X4)
-                rhs = v_w[h, g].bitcast(FP4X4)
-                rhs_scale = v_s[g][:, h * W : (h + 1) * W]
+                rhs = v_w[h, g][:, 2 * j0 : 2 * (j0 + width)].bitcast(FP4X4)
+                rhs_scale = v_s[g][:, h * W + j0 : h * W + j0 + width]
             else:
                 lhs = wb_p[a][:, 2 * t * P : 2 * (t + 1) * P].bitcast(FP4X4)
                 rhs = g_w2[h][:].bitcast(FP8X4)
                 rhs_scale = g_s2[h][:]
             nc.tensor.matmul_mx(
-                out=z[h, a, t][:],
+                out=z[h, a, t][:, js],
                 lhsT=lhs,
                 lhsT_scale=ws_p[g, a][:, m],
                 rhs=rhs,
                 rhs_scale=rhs_scale,
-                start=(g == first),
+                start=(g == first and j0 == 0),
                 stop=(g == final),
             )
             if g == final:
@@ -227,19 +237,33 @@ def tile_list_kg_tanh_bias_kernel(
                 stop=stop,
             )
 
-        accs = {}
-
-        def score_first(a):
+        def score_first():
             for c in range(4):
-                if a == 0:
-                    accs[c] = bank(c)
-                score_pass(accs[c][:], 0, a, c, slice(0, W), a == 0, a == 1)
-                if a == 1:
-                    y = new([P, W], F32, f"y0{c}")
-                    nc.scalar.activation(out=y[:], in_=accs[c][:], func=ACT.Identity, bias=b_sb[:, c : c + 1])
-                    nc.sync.dma_start(out[c * P : (c + 1) * P, 0:W], y[:])
+                acc = bank(c)
+                for a in range(2):
+                    score_pass(acc[:], 0, a, c, slice(0, W), a == 0, a == 1)
+                y = new([P, W], F32, f"y0{c}")
+                nc.scalar.activation(out=y[:], in_=acc[:], func=ACT.Identity, bias=b_sb[:, c : c + 1])
+                nc.sync.dma_start(out[c * P : (c + 1) * P, 0:W], y[:])
 
+        quarter = []
         piece = {}
+
+        def score_quarter(a):
+            for v in range(2):
+                if a == 0:
+                    quarter.append(bank(4 + v)[:].rearrange("p (e j) -> p e j", e=2))
+                for e in range(2):
+                    score_pass(quarter[v][:, e, :], 1, a, 2 * v + e, slice(0, half), (a, e) == (0, 0), (a, e) == (1, 1))
+
+        def store_quarter(v):
+            y = new([P, 2, half], F32, f"y_quarter{v}")
+            if v == 1:
+                nc.vector.tensor_tensor(y[:], quarter[v], b_sb[:, 2:4].unsqueeze(2).to_broadcast([P, 2, half]), ALU.add)
+            else:
+                for e in range(2):
+                    nc.scalar.activation(out=y[:, e, :], in_=quarter[v][:, e, :], func=ACT.Identity, bias=b_sb[:, e : e + 1])
+            nc.sync.dma_start(out[2 * v * P : 2 * (v + 1) * P, W : W + half].rearrange("(e p) j -> p e j", p=P), y[:])
 
         def score_piece(k, a):
             if a == 0:
@@ -249,7 +273,7 @@ def tile_list_kg_tanh_bias_kernel(
 
         def store_piece(k):
             y = new([P, 4, P], F32, f"y1{k}")
-            if k >= 2:
+            if k == 3:
                 nc.vector.tensor_tensor(y[:], piece[k], b_sb[:].unsqueeze(2).to_broadcast([P, 4, P]), ALU.add)
             else:
                 for c in range(4):
@@ -257,42 +281,33 @@ def tile_list_kg_tanh_bias_kernel(
             nc.sync.dma_start(out[:, W + k * P : W + (k + 1) * P].rearrange("(c p) j -> p c j", p=P), y[:])
 
         gather1_scales()
-        nc.sync.dma_start(wa_w[0, 1], wa_i[:, 1, 0:W])
-        load_rows(tab2_s, tab2_rows, [2, 3], 32)
-        nc.sync.dma_start(wb_w[:], wb_words[0].bitcast(I32))
-        load_rows(wb_s, wb_rows, range(4), 32)
-        wa_w1 = new([P, 2, W], I32, "wa_w1")
-        nc.sync.dma_start(wa_w1[:], wa_i[:, :, W : 2 * W])
-        for g in range(2):
-            wa_w[1, g] = wa_w1[:, g, :]
-        nc.sync.dma_start(sm_sb[:], sm.rearrange("(a p t) -> p a t", a=2, t=4))
-        gather1_words(0)
-        part(0, 0)
-        part(0, 1)
+        half = W // 2
         permute_wa(0, 0)
         permute_scales(0, 0, wa_s[:, 0, :])
+        for j0 in (0, half):
+            gather1_words(0, j0, half)
+            part(0, j0, half)
+            for t in range(4):
+                one_pass(0, 0, t, 0, j0, half)
         permute_wa(0, 1)
         permute_scales(1, 0, wa_s[:, 1, :])
         gather1_words(1)
-        part_both(1)
-        for g in range(2):
-            for h in range(2):
-                passes(h, 0, [(t, g) for t in range(4)])
+        part(1)
+        for h, g in ((0, 1), (1, 0), (1, 1)):
+            passes(h, 0, [(t, g) for t in range(4)])
         gather2_words(0)
         gather2_scales(0)
         for a in range(2):
             permute_wb(a)
-        permute_scales(2, 0, wb_s[:])
+            permute_scales(2, a, wb_s[:])
         passes(0, 0, [(t, 2) for t in range(4)])
-        gather2_words(1)
-        gather2_scales(1)
-        passes(1, 0, [(t, 2) for t in range(4)])
         for g in range(2):
             permute_scales(g, 1, wa_s[:, g, :])
-        permute_scales(2, 1, wb_s[:])
-        for g in range(2):
             permute_wa(1, g)
-        passes(0, 1, [(t, 2) for t in range(4)] + [(t, g) for t in range(4) for g in range(2)])
+        gather2_words(1)
+        gather2_scales(1)
+        passes(0, 1, [(t, g) for t in range(4) for g in (2, 0, 1)])
+        passes(1, 0, [(t, 2) for t in range(4)])
         en_s = new([P, 2, N // 4], I32, "en_s")
         en_w = new([P, 2, N // 2], I32, "en_w")
         nc.sync.dma_start(en_w[:], en_words.rearrange("a p n -> p a n").bitcast(I32))
@@ -302,27 +317,24 @@ def tile_list_kg_tanh_bias_kernel(
         with nc.allow_non_contiguous_dma(reason="one bias value to a partition"):
             nc.sync.dma_start(b_sb[:], b.rearrange("(c p) -> p c", p=P))
         passes(1, 1, [(t, g) for t in range(4) for g in (2, 0, 1)])
-        half = W // 2
         scale_planes(1, 1, half, half)
-        for step in (smooth, quantise):
-            for j0 in (0, half):
-                step(0, 0, j0, half)
-        for j0 in (0, half):
-            smooth(1, 0, j0, half)
-        for step in (smooth, quantise):
-            for j0 in (0, half):
-                step(0, 1, j0, half)
-        for j0 in (0, half):
-            quantise(1, 0, j0, half)
-        for a in range(2):
-            score_first(a)
-        for k in range(4):
+        for h, a in ((0, 0), (0, 1), (1, 0)):
+            for step in (smooth, quantise):
+                for j0 in (0, half):
+                    step(h, a, j0, half)
+        score_first()
+        score_quarter(0)
+        for k in (2, 3):
             score_piece(k, 0)
-        smooth(1, 1, 0, P)
-        for k in range(4):
-            if k < 3:
-                (smooth if k == 0 else weave)(1, 1, (k + 1) * P, P)
+        smooth(1, 1, 0, half)
+        weave(1, 1, 2 * P, P)
+        quantise(1, 1, 0, half)
+        score_quarter(1)
+        weave(1, 1, 3 * P, P)
+        for k in (2, 3):
             quantise(1, 1, k * P, P)
             score_piece(k, 1)
-        for k in range(4):
+        for v in range(2):
+            store_quarter(v)
+        for k in (2, 3):
             store_piece(k)

@@ -19,7 +19,7 @@ ALU = mybir.AluOpType
 P = 128
 W = 512
 PLACE = {
-    "g_w0_0": 512, "g_w0_256": 0, "g_w1_0": 1024,
+    "wa_s": 0, "g_w1_0": 0,
     "wa_w1": 4096, "g_w21": 4096, "g_s21": 6144,
     "tab_w": 16384, "g_w20": 16384, "g_s20": 18432,
 }
@@ -133,7 +133,7 @@ def tile_list_kg_tanh_bias_kernel(
 
         def permute_scales(g, a, src):
             ws_p[g, a] = new([P, W], U8, f"ws_p{g}{a}")
-            nc.gpsimd.tensor_copy(
+            nc.vector.tensor_copy(
                 ws_p[g, a][:].rearrange("p (t c i) -> p c t i", t=4, i=16),
                 src.bitcast(U8)[:, a * W : (a + 1) * W].rearrange("p (c i t) -> p c t i", t=4, i=16),
             )
@@ -287,13 +287,13 @@ def tile_list_kg_tanh_bias_kernel(
         for j0 in (0, half):
             gather1_words(0, j0, half)
             part(0, j0, half)
-            for t in range(4):
-                one_pass(0, 0, t, 0, j0, half)
         permute_wa(0, 1)
         permute_scales(1, 0, wa_s[:, 1, :])
+        for g in range(2):
+            permute_scales(g, 1, wa_s[:, g, :])
         gather1_words(1)
         part(1)
-        for h, g in ((0, 1), (1, 0), (1, 1)):
+        for h, g in ((0, 0), (0, 1), (1, 0), (1, 1)):
             passes(h, 0, [(t, g) for t in range(4)])
         gather2_words(0)
         gather2_scales(0)
@@ -302,7 +302,6 @@ def tile_list_kg_tanh_bias_kernel(
             permute_scales(2, a, wb_s[:])
         passes(0, 0, [(t, 2) for t in range(4)])
         for g in range(2):
-            permute_scales(g, 1, wa_s[:, g, :])
             permute_wa(1, g)
         gather2_words(1)
         gather2_scales(1)

@@ -246,39 +246,24 @@ def tile_list_kg_tanh_bias_kernel(
                 nc.scalar.activation(out=y[:], in_=acc[:], func=ACT.Identity, bias=b_sb[:, c : c + 1])
                 nc.sync.dma_start(out[c * P : (c + 1) * P, 0:W], y[:])
 
-        quarter = []
-        piece = {}
+        quarter = {}
 
-        def score_quarter(a):
+        def score_quarter(q, a):
             for v in range(2):
                 if a == 0:
-                    quarter.append(bank(4 + v)[:].rearrange("p (e j) -> p e j", e=2))
+                    quarter[q, v] = bank(4 + 2 * q + v)[:].rearrange("p (e j) -> p e j", e=2)
                 for e in range(2):
-                    score_pass(quarter[v][:, e, :], 1, a, 2 * v + e, slice(0, half), (a, e) == (0, 0), (a, e) == (1, 1))
+                    score_pass(quarter[q, v][:, e, :], 1, a, 2 * v + e, slice(q * half, (q + 1) * half), (a, e) == (0, 0), (a, e) == (1, 1))
 
-        def store_quarter(v):
-            y = new([P, 2, half], F32, f"y_quarter{v}")
+        def store_quarter(q, v):
+            y = new([P, 2, half], F32, f"y_quarter{q}{v}")
             if v == 1:
-                nc.vector.tensor_tensor(y[:], quarter[v], b_sb[:, 2:4].unsqueeze(2).to_broadcast([P, 2, half]), ALU.add)
+                nc.vector.tensor_tensor(y[:], quarter[q, v], b_sb[:, 2:4].unsqueeze(2).to_broadcast([P, 2, half]), ALU.add)
             else:
                 for e in range(2):
-                    nc.scalar.activation(out=y[:, e, :], in_=quarter[v][:, e, :], func=ACT.Identity, bias=b_sb[:, e : e + 1])
-            nc.sync.dma_start(out[2 * v * P : 2 * (v + 1) * P, W : W + half].rearrange("(e p) j -> p e j", p=P), y[:])
-
-        def score_piece(k, a):
-            if a == 0:
-                piece[k] = bank(4 + k)[:].rearrange("p (c j) -> p c j", c=4)
-            for c in range(4):
-                score_pass(piece[k][:, c, :], 1, a, c, slice(k * P, (k + 1) * P), (a, c) == (0, 0), (a, c) == (1, 3))
-
-        def store_piece(k):
-            y = new([P, 4, P], F32, f"y1{k}")
-            if k == 3:
-                nc.vector.tensor_tensor(y[:], piece[k], b_sb[:].unsqueeze(2).to_broadcast([P, 4, P]), ALU.add)
-            else:
-                for c in range(4):
-                    nc.scalar.activation(out=y[:, c, :], in_=piece[k][:, c, :], func=ACT.Identity, bias=b_sb[:, c : c + 1])
-            nc.sync.dma_start(out[:, W + k * P : W + (k + 1) * P].rearrange("(c p) j -> p c j", p=P), y[:])
+                    nc.scalar.activation(out=y[:, e, :], in_=quarter[q, v][:, e, :], func=ACT.Identity, bias=b_sb[:, e : e + 1])
+            first = W + q * half
+            nc.sync.dma_start(out[2 * v * P : 2 * (v + 1) * P, first : first + half].rearrange("(e p) j -> p e j", p=P), y[:])
 
         gather1_scales()
         half = W // 2
@@ -322,18 +307,13 @@ def tile_list_kg_tanh_bias_kernel(
                 for j0 in (0, half):
                     step(h, a, j0, half)
         score_first()
-        score_quarter(0)
-        for k in (2, 3):
-            score_piece(k, 0)
+        for q in range(2):
+            score_quarter(q, 0)
         smooth(1, 1, 0, half)
-        weave(1, 1, 2 * P, P)
-        quantise(1, 1, 0, half)
-        score_quarter(1)
-        weave(1, 1, 3 * P, P)
-        for k in (2, 3):
-            quantise(1, 1, k * P, P)
-            score_piece(k, 1)
-        for v in range(2):
-            store_quarter(v)
-        for k in (2, 3):
-            store_piece(k)
+        weave(1, 1, half, half)
+        for q in range(2):
+            quantise(1, 1, q * half, half)
+            score_quarter(q, 1)
+        for q in range(2):
+            for v in range(2):
+                store_quarter(q, v)

@@ -237,8 +237,8 @@ def tile_list_kg_tanh_bias_kernel(
                 stop=stop,
             )
 
-        def score_first():
-            for c in range(4):
+        def score_first(rows):
+            for c in rows:
                 acc = bank(c)
                 for a in range(2):
                     score_pass(acc[:], 0, a, c, slice(0, W), a == 0, a == 1)
@@ -301,12 +301,13 @@ def tile_list_kg_tanh_bias_kernel(
         with nc.allow_non_contiguous_dma(reason="one bias value to a partition"):
             nc.sync.dma_start(b_sb[:], b.rearrange("(c p) -> p c", p=P))
         passes(1, 1, [(t, g) for t in range(4) for g in (2, 0, 1)])
-        scale_planes(1, 1, half, half)
         for h, a in ((0, 0), (0, 1), (1, 0)):
             for step in (smooth, quantise):
                 for j0 in (0, half):
                     step(h, a, j0, half)
-        score_first()
+        score_first(range(1))
+        scale_planes(1, 1, half, half)
+        score_first(range(1, 4))
         for q in range(2):
             score_quarter(q, 0)
         smooth(1, 1, 0, half)

from contextlib import ExitStack

import concourse.mybir as mybir

K, L, R, N, T, J = 1024, 512, 1024, 512, 2048, 1024
FLOPS = 2 * J * R * (K + L + N)

F32 = mybir.dt.float32
BF16 = mybir.dt.bfloat16
I32 = mybir.dt.int32
U32 = mybir.dt.uint32
U16 = mybir.dt.uint16
U8 = mybir.dt.uint8
FP8X4 = mybir.dt.float8_e4m3fn_x4
FP4X4 = mybir.dt.float4_e2m1fn_x4
ACT = mybir.ActivationFunctionType
ALU = mybir.AluOpType

P = 128
W = 512
PLACE = {
    "wa_s": 0, "g_w1_0": 0,
    "wa_w1": 4096, "g_w21": 4096, "g_s21": 6144,
    "tab_w": 16384, "g_w20": 16384, "g_s20": 18432,
}


def tile_list_kg_tanh_bias_kernel(
    tc, tab_words, tab_scales, tab2_words, tab2_scales, wa_words, wa_scales, wb_words, wb_scales,
    sm, en_words, en_scales, b, offs, offs2, out,
):
    nc = tc.nc
    with ExitStack() as ctx:
        keep = ctx.enter_context(tc.tile_pool(name="keep", bufs=1))
        reuse = ctx.enter_context(tc.tile_pool(name="reuse", bufs=1))
        psum = ctx.enter_context(tc.psum_pool(name="psum", bufs=1))

        def new(shape, dtype, name):
            if name in PLACE:
                return reuse.tile(shape, dtype, name=name, offset=PLACE[name], align_bytes=64)
            return keep.tile(shape, dtype, name=name, align_bytes=64)

        def bank(i):
            return psum.tile([P, W], F32, name=f"bank{i}")

        list1 = keep.tile([P, J // 16], U16, name="list1")
        list2 = keep.tile([P, J // 16], U16, name="list2")
        sm_sb = new([P, 2, 4], F32, "sm_sb")
        tab_s = new([P, T // 4], I32, "tab_s")
        tab2_s = new([P, T // 4], I32, "tab2_s")
        wa_s = new([P, 2, R // 4], I32, "wa_s")
        wb_s = new([P, R // 4], I32, "wb_s")
        tab_w = new([P, T], I32, "tab_w")
        tab2_w = new([P, T], I32, "tab2_w")
        wa_w = {(0, g): new([P, W], I32, f"wa_w0{g}")[:] for g in range(2)}
        wb_w = new([P, R // 2], I32, "wb_w")

        nc.gpsimd.memset(tab_s[:], 0)
        nc.vector.memset(wa_s[:], 0)
        nc.vector.memset(tab2_s[:], 0)
        nc.vector.memset(wb_s[:], 0)

        wa_i = wa_words.rearrange("a p r i -> p a (r i)").bitcast(I32)

        def load_rows(dst, src, step):
            for r in range(4):
                nc.sync.dma_start(dst[r:P:step], src[r].bitcast(I32))

        tab_rows = tab_scales.rearrange("a (q r) t -> r q a t", r=4)
        tab2_rows = tab2_scales[0].rearrange("(q r) t -> r q t", r=4)
        wa_rows = wa_scales.rearrange("a (q r) n -> r q a n", r=4)
        wb_rows = wb_scales[0].rearrange("(q r) n -> r q n", r=4)
        nc.sync.dma_start(list1[:], offs)
        nc.sync.dma_start(wa_w[0, 0], wa_i[:, 0, 0:W])
        load_rows(tab_s, tab_rows, 16)
        nc.sync.dma_start(tab_w[:], tab_words[0].rearrange("p t i -> p (t i)").bitcast(I32))
        load_rows(wa_s, wa_rows, 32)
        nc.sync.dma_start(wa_w[0, 1], wa_i[:, 1, 0:W])
        nc.sync.dma_start(tab2_w[:], tab2_words[0].rearrange("p t i -> p (t i)").bitcast(I32))
        nc.sync.dma_start(list2[:], offs2)
        load_rows(tab2_s, tab2_rows, 32)
        nc.sync.dma_start(wb_w[:], wb_words[0].bitcast(I32))
        load_rows(wb_s, wb_rows, 32)
        wa_w1 = new([P, 2, W], I32, "wa_w1")
        nc.sync.dma_start(wa_w1[:], wa_i[:, :, W : 2 * W])
        for g in range(2):
            wa_w[1, g] = wa_w1[:, g, :]
        nc.sync.dma_start(sm_sb[:], sm.rearrange("(a p t) -> p a t", a=2, t=4))

        moved_s = new([P, J // 4], I32, "moved_s")

        g_s = new([P, J], U8, "g_s")
        v_s = [g_s[:], moved_s[:].bitcast(U8)]
        g_s2 = {}
        g_w = {}
        g_w2 = {}
        v_w = {}

        def gather2_words(h):
            cols = slice(h * W // 16, (h + 1) * W // 16)
            g_w2[h] = new([P, W], U32, f"g_w2{h}")
            nc.vector.tensor_copy(g_w2[h][:], tab2_w[:].bitcast(U32).indirect(list2[:, cols]))

        def gather2_scales(h):
            cols = slice(h * W // 16, (h + 1) * W // 16)
            g_s2[h] = new([P, W], U8, f"g_s2{h}")
            nc.vector.tensor_copy(g_s2[h][:], tab2_s[:].bitcast(U8).indirect(list2[:, cols]))

        def gather1_scales():
            nc.vector.tensor_copy(g_s[:], tab_s[:].bitcast(U8).indirect(list1[:]))
            nc.scalar.dma_start(moved_s[0:100, :], g_s[16:116, :].bitcast(I32))

        def gather1_words(h, j0=0, width=W):
            first = h * W + j0
            g_w[h, j0] = new([P, width], U32, f"g_w{h}_{j0}")
            nc.vector.tensor_copy(g_w[h, j0][:], tab_w[:].bitcast(U32).indirect(list1[:, first // 16 : (first + width) // 16]))

        parted = {}

        def part(h, j0=0, width=W):
            if h not in parted:
                parted[h] = new([P, 2, 2 * W], U8, f"v_w{h}")
                for d in range(2):
                    v_w[h, d] = parted[h][:, d, :]
            nc.vector.tensor_copy(
                parted[h][:].bitcast(U16)[:, :, j0 : j0 + width],
                g_w[h, j0][:].bitcast(U16).rearrange("p (j d) -> p d j", d=2),
            )

        wa_p = {}
        wb_p = {}
        ws_p = {}

        def permute_scales(g, a, src):
            ws_p[g, a] = new([P, W], U8, f"ws_p{g}{a}")
            nc.vector.tensor_copy(
                ws_p[g, a][:].rearrange("p (t c i) -> p c t i", t=4, i=16),
                src.bitcast(U8)[:, a * W : (a + 1) * W].rearrange("p (c i t) -> p c t i", t=4, i=16),
            )

        def permute_wb(a):
            wb_p[a] = new([P, 2 * W], U8, f"wb_p{a}")
            nc.scalar.copy(
                wb_p[a][:].bitcast(U16).rearrange("p (t c i) -> p c t i", t=4, i=8),
                wb_w[:].bitcast(U16)[:, a * W : (a + 1) * W].rearrange("p (c i t) -> p c t i", t=4, i=8),
            )

        def permute_wa(a, g):
            wa_p[a, g] = new([P, W], U32, f"wa_p{a}{g}")
            (nc.scalar.copy if a == 0 else nc.vector.tensor_copy)(
                wa_p[a, g][:].rearrange("p (t c i) -> p c t i", t=4, i=4),
                wa_w[a, g].bitcast(U32).rearrange("p (c i t) -> p c t i", t=4, i=4),
            )

        th = {}
        hb = {}
        hq = {}
        hs = {}
        z = {}

        def one_pass(h, a, t, g, j0=0, width=W):
            m = slice(t * P, (t + 1) * P)
            js = slice(j0, j0 + width)
            first, final = (0, 2) if a == 0 else (2, 1)
            if g == first and j0 == 0:
                z[h, a, t] = bank(4 * h + t)
            if g < 2:
                lhs = wa_p[a, g][:, m].bitcast(FP8X4)
                rhs = v_w[h, g][:, 2 * j0 : 2 * (j0 + width)].bitcast(FP4X4)
                rhs_scale = v_s[g][:, h * W + j0 : h * W + j0 + width]
            else:
                lhs = wb_p[a][:, 2 * t * P : 2 * (t + 1) * P].bitcast(FP4X4)
                rhs = g_w2[h][:].bitcast(FP8X4)
                rhs_scale = g_s2[h][:]
            nc.tensor.matmul_mx(
                out=z[h, a, t][:, js],
                lhsT=lhs,
                lhsT_scale=ws_p[g, a][:, m],
                rhs=rhs,
                rhs_scale=rhs_scale,
                start=(g == first and j0 == 0),
                stop=(g == final),
            )
            if g == final:
                nc.scalar.activation(out=th[h, a][:, t, :], in_=z[h, a, t][:], func=ACT.Tanh)

        def passes(h, a, order):
            if (h, a) not in th:
                th[h, a] = new([P, 4, W], F32, f"th{h}{a}")
            for t, g in order:
                one_pass(h, a, t, g)

        def smooth(h, a, j0=0, width=W):
            hb[h, a, j0] = new([P, 4 * width], BF16, f"hb{h}{a}_{j0}")
            nc.vector.tensor_tensor(
                hb[h, a, j0][:].rearrange("p (c i t) -> p c t i", t=4, i=2),
                th[h, a][:, :, j0 : j0 + width].rearrange("p t (c i) -> p c t i", i=2),
                sm_sb[:, a, :].unsqueeze(1).unsqueeze(3).to_broadcast([P, width // 2, 4, 2]),
                ALU.mult,
            )

        planes = {}

        def scale_planes(h, a, j0, width):
            planes[h, a] = (j0, new([P, 4, width], BF16, f"planes{h}{a}"))
            for t in range(4):
                nc.scalar.activation(
                    out=planes[h, a][1][:, t, :], in_=th[h, a][:, t, j0 : j0 + width], func=ACT.Copy, scale=sm_sb[:, a, t : t + 1]
                )

        def weave(h, a, j0, width):
            first, src = planes[h, a]
            hb[h, a, j0] = new([P, 4 * width], BF16, f"hb{h}{a}_{j0}")
            nc.vector.tensor_copy(
                hb[h, a, j0][:].rearrange("p (c i t) -> p c t i", t=4, i=4),
                src[:, :, j0 - first : j0 - first + width].rearrange("p t (c i) -> p c t i", i=4),
            )

        def quantise(h, a, j0=0, width=W):
            if (h, a) not in hq:
                hq[h, a] = new([P, W], U32, f"hq{h}{a}")
                hs[h, a] = new([P, W], U8, f"hs{h}{a}")
            nc.vector.quantize_mx(
                out=hq[h, a][:, j0 : j0 + width].bitcast(FP8X4),
                scales=hs[h, a][:, j0 : j0 + width],
                in_=hb[h, a, j0][:],
            )

        def score_pass(acc, h, a, c, cols, start, stop):
            nc.tensor.matmul_mx(
                out=acc,
                lhsT=en_w[:].bitcast(U8)[:, a, 2 * c * P : 2 * (c + 1) * P].bitcast(FP4X4),
                lhsT_scale=en_s[:].bitcast(U8)[:, a, c * P : (c + 1) * P],
                rhs=hq[h, a][:, cols].bitcast(FP8X4),
                rhs_scale=hs[h, a][:, cols],
                start=start,
                stop=stop,
            )

        def score_first(rows):
            for c in rows:
                acc = bank(c)
                for a in range(2):
                    score_pass(acc[:], 0, a, c, slice(0, W), a == 0, a == 1)
                y = new([P, W], F32, f"y0{c}")
                nc.scalar.activation(out=y[:], in_=acc[:], func=ACT.Identity, bias=b_sb[:, c : c + 1])
                nc.sync.dma_start(out[c * P : (c + 1) * P, 0:W], y[:])

        quarter = {}

        def score_quarter(q, a):
            for v in range(2):
                if a == 0:
                    quarter[q, v] = bank(4 + 2 * q + v)[:].rearrange("p (e j) -> p e j", e=2)
                for e in range(2):
                    score_pass(quarter[q, v][:, e, :], 1, a, 2 * v + e, slice(q * half, (q + 1) * half), (a, e) == (0, 0), (a, e) == (1, 1))

        def store_quarter(q, v):
            y = new([P, 2, half], F32, f"y_quarter{q}{v}")
            if v == 1:
                nc.vector.tensor_tensor(y[:], quarter[q, v], b_sb[:, 2:4].unsqueeze(2).to_broadcast([P, 2, half]), ALU.add)
            else:
                for e in range(2):
                    nc.scalar.activation(out=y[:, e, :], in_=quarter[q, v][:, e, :], func=ACT.Identity, bias=b_sb[:, e : e + 1])
            first = W + q * half
            nc.sync.dma_start(out[2 * v * P : 2 * (v + 1) * P, first : first + half].rearrange("(e p) j -> p e j", p=P), y[:])

        gather1_scales()
        half = W // 2
        permute_wa(0, 0)
        permute_scales(0, 0, wa_s[:, 0, :])
        for j0 in (0, half):
            gather1_words(0, j0, half)
            part(0, j0, half)
        permute_wa(0, 1)
        permute_scales(1, 0, wa_s[:, 1, :])
        for g in range(2):
            permute_scales(g, 1, wa_s[:, g, :])
        gather1_words(1)
        part(1)
        for h, g in ((0, 0), (0, 1), (1, 0), (1, 1)):
            passes(h, 0, [(t, g) for t in range(4)])
        gather2_words(0)
        gather2_scales(0)
        for a in range(2):
            permute_wb(a)
            permute_scales(2, a, wb_s[:])
        passes(0, 0, [(t, 2) for t in range(4)])
        for g in range(2):
            permute_wa(1, g)
        gather2_words(1)
        gather2_scales(1)
        passes(0, 1, [(t, g) for t in range(4) for g in (2, 0, 1)])
        passes(1, 0, [(t, 2) for t in range(4)])
        en_s = new([P, 2, N // 4], I32, "en_s")
        en_w = new([P, 2, N // 2], I32, "en_w")
        nc.sync.dma_start(en_w[:], en_words.rearrange("a p n -> p a n").bitcast(I32))
        for r in range(4):
            nc.sync.dma_start(en_s[r:P:32, :, :], en_scales.rearrange("a (q r) n -> r q a n", r=4)[r].bitcast(I32))
        b_sb = new([P, 4], F32, "b_sb")
        with nc.allow_non_contiguous_dma(reason="one bias value to a partition"):
            nc.sync.dma_start(b_sb[:], b.rearrange("(c p) -> p c", p=P))
        passes(1, 1, [(t, g) for t in range(4) for g in (2, 0, 1)])
        for h, a in ((0, 0), (0, 1), (1, 0)):
            for step in (smooth, quantise):
                for j0 in (0, half):
                    step(h, a, j0, half)
        score_first(range(1))
        scale_planes(1, 1, half, half)
        score_first(range(1, 4))
        for q in range(2):
            score_quarter(q, 0)
        smooth(1, 1, 0, half)
        weave(1, 1, half, half)
        for q in range(2):
            quantise(1, 1, q * half, half)
            score_quarter(q, 1)
        for q in range(2):
            for v in range(2):
                store_quarter(q, v)
